import numpy as np
import ml_dtypes


def mxq(x, axis, fmt="e4m3"):
    dtype, down = {"e4m3": (ml_dtypes.float8_e4m3fn, 7), "e5m2": (ml_dtypes.float8_e5m2, 14)}[fmt]
    v = np.moveaxis(np.asarray(x, np.float32).astype(ml_dtypes.bfloat16).astype(np.float64), axis, -1)
    blocks = v.reshape(v.shape[:-1] + (-1, 32))
    amax = np.abs(blocks).max(-1, keepdims=True)
    byte = np.maximum(np.where(amax > 0, np.frexp(amax)[1] - 1 + 127, 0) - down, 1)
    scale = np.exp2(byte - 127.0)
    codes = (blocks / scale).astype(np.float32).astype(dtype).astype(np.float64)
    return np.moveaxis((codes * scale).reshape(v.shape), -1, axis)


WIDE = False


def mx_kscale(k):
    if not WIDE:
        return np.ones(k)
    levels = np.array([10, -10, 5, -5, 0])
    if k % 512:
        return np.exp2(np.random.permutation(np.resize(levels, k // 32))).repeat(32)
    a = np.empty((k // 512, 16))
    for p in range(k // 512):
        a[p, :8] = np.random.permutation(np.resize(levels, 8))
        for g in range(8):
            far = levels[np.abs(levels - a[p, g]) >= 10]
            a[p, g + 8] = far[np.random.randint(len(far))]
    return np.exp2(a.ravel()).repeat(32)


def f64(x):
    return np.asarray(x).astype(np.float64)


def striped(idx):
    return np.tile(idx.reshape(-1, 16).T, (8, 1)).astype(np.uint16)


def unstriped(offs):
    return offs[:16].T.reshape(-1).astype(np.int64)


def pack_weight(w):
    k, n = w.shape
    w = f64(np.asarray(w, np.float32).astype(ml_dtypes.bfloat16)).reshape(k // 32, 32, n)
    amax = np.abs(w).max(1)
    byte = np.clip(np.where(amax > 0, np.frexp(amax)[1] - 1 + 127 - 7, 1), 1, 254)
    scaled = (w * np.exp2(127.0 - byte)[:, None, :]).reshape(k, n).astype(np.float32)
    words = np.ascontiguousarray(scaled.reshape(k // 512, 128, 4, n).transpose(0, 1, 3, 2)).astype(ml_dtypes.float8_e4m3fn).view(np.uint8)
    return words, np.ascontiguousarray(byte.astype(np.uint8).reshape(k // 512, 16, n))


def unpack_weight(words, scales):
    g, p, n, _ = words.shape
    vals = np.ascontiguousarray(words).view(ml_dtypes.float8_e4m3fn).astype(np.float64) * np.repeat(np.exp2(scales.astype(np.float64) - 127.0), 8, axis=1)[..., None]
    return vals.transpose(0, 1, 3, 2).reshape(g * 512, n)


K, T, S, V, R, W = 1024, 4096, 1024, 512, 256, 1024


def setup_inputs():
    n = np.random.standard_normal
    s = mx_kscale(K)[:, None]
    packed_xT = pack_weight(n((K, T)) * s)
    packed_eT = pack_weight(n((K, W)) * s)
    return {
        "x_words": packed_xT[0],
        "x_scales": packed_xT[1],
        "hT": (n((K, V)) / np.sqrt(K) / s).astype(np.float32),
        "e_words": packed_eT[0],
        "e_scales": packed_eT[1],
        "offs": striped(np.random.permutation(T)[:S]),
        "cent": striped(np.random.permutation(W)[:R]),
        "cell": striped(np.random.permutation(np.concatenate([np.arange(R), np.random.randint(0, R, S - R)]))),
    }


def reference(x_words, x_scales, hT, e_words, e_scales, offs, cent, cell):
    hTq = mxq(f64(hT), 0, "e4m3")
    xq = unpack_weight(x_words, x_scales)[:, unstriped(offs)]
    y = hTq.T @ xq
    e_cent = unpack_weight(e_words, e_scales)[:, unstriped(cent)]
    z = hTq.T @ e_cent
    return y + z[:, unstriped(cell)]

@@ -1,0 +1,166 @@
+from contextlib import ExitStack
+
+import concourse.mybir as mybir
+
+K, T, S, V, R, W = 1024, 4096, 1024, 512, 256, 1024
+FLOPS = 2 * K * V * (S + R)
+
+F32 = mybir.dt.float32
+BF16 = mybir.dt.bfloat16
+I32 = mybir.dt.int32
+U32 = mybir.dt.uint32
+U16 = mybir.dt.uint16
+U8 = mybir.dt.uint8
+FP8X4 = mybir.dt.float8_e4m3fn_x4
+ADD = mybir.AluOpType.add
+
+P = 128
+PACK = 4
+PASSES = 2
+BLOCKS = 4
+HALF = 512
+HALVES = 2
+Z_WINDOW = 544
+EARLY = 2
+
+
+def tile_picked_yivf_sum_p_kernel(
+    tc, x_words, x_scales, hT, e_words, e_scales, offs, cent, cell, out
+):
+    nc = tc.nc
+    with ExitStack() as ctx:
+        keep = ctx.enter_context(tc.tile_pool(name="keep", bufs=1))
+        psum = ctx.enter_context(tc.psum_pool(name="psum", bufs=1))
+
+        offs_t = keep.tile([P, S // 16], U16, name="offs_t")
+        cent_t = keep.tile([P, R // 16], U16, name="cent_t")
+        cell_t = keep.tile([P, S // 16], U16, name="cell_t")
+        x_tab = [keep.tile([P, T], I32, name="x_tab%d" % o, align_bytes=64) for o in range(PASSES)]
+        e_tab = keep.tile([P, PASSES, W], I32, name="e_tab", align_bytes=64)
+        xs_tab = keep.tile([P, T], U8, name="xs_tab", tag="xs_tab", align_bytes=64)
+        es_tab = keep.tile([P, W], U8, name="es_tab", align_bytes=64)
+        h_raw = [[keep.tile([P, PACK, 2 * P], F32, name="h_raw%d%d" % (g, o), align_bytes=64) for o in range(PASSES)] for g in range(2)]
+        z_win = [keep.tile([P, Z_WINDOW], F32, name="z_win%d" % b, align_bytes=64) for b in range(BLOCKS)]
+
+        nc.vector.memset(xs_tab[:].bitcast(I32), 0)
+        nc.gpsimd.memset(es_tab[:].bitcast(I32), 0)
+        for b in range(BLOCKS):
+            nc.gpsimd.memset(z_win[b][:, R:], 0.0)
+
+        def load_scales(queue, tab, src):
+            for q in range(4):
+                queue.dma_start(out=tab[32 * q : 32 * q + 8, :].bitcast(I32), in_=src[:, 4 * q : 4 * q + 4, :].bitcast(I32))
+
+        def load_h(g, o):
+            rows = hT[512 * o : 512 * (o + 1), 2 * P * g : 2 * P * (g + 1)]
+            nc.sync.dma_start(out=h_raw[g][o][:], in_=rows.rearrange("(p j) c -> p j c", j=PACK))
+
+        def load_x(o):
+            nc.sync.dma_start(out=x_tab[o][:], in_=x_words[o].rearrange("p n t -> p (n t)").bitcast(I32))
+
+        nc.sync.dma_start(cent_t[:], cent)
+        nc.sync.dma_start(offs_t[:], offs)
+        load_scales(nc.scalar, es_tab, e_scales)
+        load_scales(nc.gpsimd, xs_tab, x_scales)
+        nc.sync.dma_start(out=e_tab[:], in_=e_words.rearrange("o p n t -> p o (n t)").bitcast(I32))
+        load_h(0, 0)
+        load_h(0, 1)
+        load_x(0)
+        nc.sync.dma_start(cell_t[:], cell)
+        load_x(1)
+        load_h(1, 0)
+        load_h(1, 1)
+
+        xs_got = keep.tile([P, S], U8, name="xs_got", align_bytes=64)
+        es_got = keep.tile([P, R], U8, name="es_got", align_bytes=64)
+        e_got = [keep.tile([P, R], U32, name="e_got%d" % o, align_bytes=64) for o in range(PASSES)]
+        x_got = [[keep.tile([P, HALF], U32, name="x_got%d%d" % (o, s), align_bytes=64) for s in range(HALVES)] for o in range(PASSES)]
+        h_codes = {}
+        h_scales = [keep.tile([P, PASSES * P], U8, name="h_scales%d" % b, align_bytes=64) for b in range(BLOCKS)]
+
+        def half_list(t, s):
+            return t[:, s * HALF // 16 : (s + 1) * HALF // 16]
+
+        def gather_x(o):
+            for s in range(HALVES):
+                nc.vector.tensor_copy(x_got[o][s][:], x_tab[o][:].bitcast(U32).indirect(half_list(offs_t, s)))
+
+        def quantise_h(b):
+            grouped = keep.tile([P, PASSES, P * PACK], BF16, name="grouped%d" % b, tag="grouped%d" % b, align_bytes=64)
+            for o in range(PASSES):
+                src = h_raw[b // 2][o][:, :, (b % 2) * P : (b % 2 + 1) * P]
+                nc.scalar.copy(
+                    grouped[:, o, :].rearrange("p (c i j) -> p c j i", i=4, j=PACK),
+                    src.rearrange("p j (c i) -> p c j i", i=4),
+                )
+            h_codes[b] = keep.tile([P, PASSES * P], U32, name="h_codes%d" % b, tag="xs_tab" if b == 0 else "h_codes%d" % b, align_bytes=64)
+            nc.vector.quantize_mx(h_codes[b][:].bitcast(FP8X4), h_scales[b][:], grouped[:].rearrange("p o n -> p (o n)"))
+
+        def one_pass(acc, b, o, codes, scales):
+            nc.tensor.matmul_mx(
+                acc,
+                lhsT=h_codes[b][:, o * P : (o + 1) * P].bitcast(FP8X4),
+                lhsT_scale=h_scales[b][:, o * P : (o + 1) * P],
+                rhs=codes.bitcast(FP8X4),
+                rhs_scale=scales,
+                start=(o == 0),
+                stop=(o == PASSES - 1),
+            )
+
+        def cell_scores(b, bank):
+            acc = psum.tile([P, R], F32, name="z%d" % b, tag="bank%d" % bank)
+            for o in range(PASSES):
+                one_pass(acc[:], b, o, e_got[o][:], es_got[4 * o : P, :])
+            nc.scalar.copy(z_win[b][:, :R], acc[:])
+
+        def y_pass(acc, b, s, o):
+            one_pass(acc[:], b, o, x_got[o][s][:], xs_got[4 * o : P, s * HALF : (s + 1) * HALF])
+
+        def store(b, s, res):
+            nc.sync.dma_start(out=out[b * P : (b + 1) * P, s * HALF : (s + 1) * HALF], in_=res[:])
+
+        nc.vector.tensor_copy(es_got[:], es_tab[:].indirect(cent_t[:]))
+        for o in range(PASSES):
+            nc.vector.tensor_copy(e_got[o][:], e_tab[:, o, :].bitcast(U32).indirect(cent_t[:]))
+        nc.vector.tensor_copy(xs_got[:], xs_tab[:].indirect(offs_t[:]))
+
+        z_got = {}
+        for b in range(EARLY):
+            quantise_h(b)
+            cell_scores(b, b % 2)
+            for s in range(HALVES):
+                z_got[b, s] = keep.tile([P, HALF], F32, name="z_got%d%d" % (b, s))
+                nc.vector.tensor_copy(z_got[b, s][:], z_win[b][:].indirect(half_list(cell_t, s)))
+        gather_x(0)
+
+        y_acc = {}
+        for s in range(HALVES):
+            for b in range(EARLY):
+                y_acc[b, s] = psum.tile([P, HALF], F32, name="y%d%d" % (b, s), tag="bank%d" % (2 + 2 * b + s))
+                y_pass(y_acc[b, s], b, s, 0)
+        gather_x(1)
+        for s in range(HALVES):
+            for b in range(EARLY):
+                y_pass(y_acc[b, s], b, s, 1)
+        for s in range(HALVES):
+            if s == 1:
+                quantise_h(EARLY)
+            for b in range(EARLY):
+                res = keep.tile([P, HALF], F32, name="res%d%d" % (b, s), tag="grouped%d" % EARLY if (b, s) == (0, 1) else "res%d%d" % (b, s), align_bytes=64)
+                nc.vector.tensor_tensor(res[:], y_acc[b, s][:], z_got[b, s][:], ADD)
+                store(b, s, res)
+
+        late_banks = {2: (6, 0, 1), 3: (7, 6, 2)}
+        for b in range(EARLY, BLOCKS):
+            if b > EARLY:
+                quantise_h(b)
+            cell_scores(b, late_banks[b][0])
+            for s in range(HALVES):
+                acc = psum.tile([P, HALF], F32, name="y%d%d" % (b, s), tag="bank%d" % late_banks[b][1 + s])
+                for o in range(PASSES):
+                    y_pass(acc, b, s, o)
+                y_sb = keep.tile([P, HALF], F32, name="y_sb%d%d" % (b, s))
+                nc.scalar.copy(y_sb[:], acc[:])
+                res = keep.tile([P, HALF], F32, name="res%d%d" % (b, s))
+                nc.vector.tensor_tensor(res[:], z_win[b][:].indirect(half_list(cell_t, s)), y_sb[:], ADD)
+                store(b, s, res)

@@ -21,7 +21,8 @@ BLOCKS = 4
 HALF = 512
 HALVES = 2
 Z_WINDOW = 544
-EARLY = 2
+EARLY = 3
+H_LOADS = [(0, 1), (1, 2), (2, 3), (3, 4)]
 
 
 def tile_picked_yivf_sum_p_kernel(
@@ -37,63 +38,77 @@ def tile_picked_yivf_sum_p_kernel(
         cell_t = keep.tile([P, S // 16], U16, name="cell_t")
         x_tab = [keep.tile([P, T], I32, name="x_tab%d" % o, align_bytes=64) for o in range(PASSES)]
         e_tab = keep.tile([P, PASSES, W], I32, name="e_tab", align_bytes=64)
-        xs_tab = keep.tile([P, T], U8, name="xs_tab", tag="xs_tab", align_bytes=64)
+        xs_tab = keep.tile([P, T], U8, name="xs_tab", align_bytes=64)
         es_tab = keep.tile([P, W], U8, name="es_tab", align_bytes=64)
-        h_raw = [[keep.tile([P, PACK, 2 * P], F32, name="h_raw%d%d" % (g, o), align_bytes=64) for o in range(PASSES)] for g in range(2)]
+        xs_got = keep.tile([P, S], U8, name="xs_got", align_bytes=64)
+        xs_mx = keep.tile([P, S], U8, name="xs_mx", align_bytes=64)
         z_win = [keep.tile([P, Z_WINDOW], F32, name="z_win%d" % b, align_bytes=64) for b in range(BLOCKS)]
 
-        nc.vector.memset(xs_tab[:].bitcast(I32), 0)
         nc.gpsimd.memset(es_tab[:].bitcast(I32), 0)
+        nc.vector.memset(xs_tab[32:64, :].bitcast(I32), 0)
+        nc.vector.memset(xs_tab[64:128, :].bitcast(I32), 0)
+        nc.gpsimd.memset(xs_mx[:].bitcast(I32), 0)
         for b in range(BLOCKS):
             nc.gpsimd.memset(z_win[b][:, R:], 0.0)
 
-        def load_scales(queue, tab, src):
-            for q in range(4):
-                queue.dma_start(out=tab[32 * q : 32 * q + 8, :].bitcast(I32), in_=src[:, 4 * q : 4 * q + 4, :].bitcast(I32))
+        h_raw = {}
 
-        def load_h(g, o):
-            rows = hT[512 * o : 512 * (o + 1), 2 * P * g : 2 * P * (g + 1)]
-            nc.sync.dma_start(out=h_raw[g][o][:], in_=rows.rearrange("(p j) c -> p j c", j=PACK))
+        def load_h(g):
+            first, last = H_LOADS[g]
+            for o in range(PASSES):
+                raw = keep.tile([P, PACK, (last - first) * P], F32, name="h_raw%d%d" % (g, o), align_bytes=64)
+                rows = hT[512 * o : 512 * (o + 1), first * P : last * P]
+                nc.sync.dma_start(out=raw[:], in_=rows.rearrange("(p j) c -> p j c", j=PACK))
+                for b in range(first, last):
+                    h_raw[b, o] = raw[:, :, (b - first) * P : (b - first + 1) * P]
 
         def load_x(o):
             nc.sync.dma_start(out=x_tab[o][:], in_=x_words[o].rearrange("p n t -> p (n t)").bitcast(I32))
 
-        nc.sync.dma_start(cent_t[:], cent)
-        nc.sync.dma_start(offs_t[:], offs)
-        load_scales(nc.scalar, es_tab, e_scales)
-        load_scales(nc.gpsimd, xs_tab, x_scales)
-        nc.sync.dma_start(out=e_tab[:], in_=e_words.rearrange("o p n t -> p o (n t)").bitcast(I32))
-        load_h(0, 0)
-        load_h(0, 1)
-        load_x(0)
-        nc.sync.dma_start(cell_t[:], cell)
-        load_x(1)
-        load_h(1, 0)
-        load_h(1, 1)
+        def place_x_scales(o):
+            for q in range(4):
+                src = 16 * o + 4 * q
+                dst = 32 * q + 4 * o
+                nc.sync.dma_start(out=xs_mx[dst : dst + 4, :].bitcast(I32), in_=xs_got[src : src + 4, :].bitcast(I32))
 
-        xs_got = keep.tile([P, S], U8, name="xs_got", align_bytes=64)
+        nc.sync.dma_start(offs_t[:], offs)
+        nc.sync.dma_start(out=xs_tab[0:32, :].bitcast(I32), in_=x_scales.rearrange("o q c -> (o q) c").bitcast(I32))
+        nc.sync.dma_start(cent_t[:], cent)
+        for q in range(4):
+            nc.scalar.dma_start(out=es_tab[32 * q : 32 * q + 8, :].bitcast(I32), in_=e_scales[:, 4 * q : 4 * q + 4, :].bitcast(I32))
+        nc.sync.dma_start(out=e_tab[:], in_=e_words.rearrange("o p n t -> p o (n t)").bitcast(I32))
+        nc.vector.tensor_copy(xs_got[:], xs_tab[:].indirect(offs_t[:]))
+        load_h(0)
+        load_h(1)
+        nc.sync.dma_start(cell_t[:], cell)
+        load_x(0)
+        place_x_scales(0)
+        load_h(2)
+        load_x(1)
+        place_x_scales(1)
+        load_h(3)
+
         es_got = keep.tile([P, R], U8, name="es_got", align_bytes=64)
         e_got = [keep.tile([P, R], U32, name="e_got%d" % o, align_bytes=64) for o in range(PASSES)]
-        x_got = [[keep.tile([P, HALF], U32, name="x_got%d%d" % (o, s), align_bytes=64) for s in range(HALVES)] for o in range(PASSES)]
-        h_codes = {}
+        x_got = {}
+        h_codes = [keep.tile([P, PASSES * P], U32, name="h_codes%d" % b, align_bytes=64) for b in range(BLOCKS)]
         h_scales = [keep.tile([P, PASSES * P], U8, name="h_scales%d" % b, align_bytes=64) for b in range(BLOCKS)]
 
         def half_list(t, s):
             return t[:, s * HALF // 16 : (s + 1) * HALF // 16]
 
-        def gather_x(o):
-            for s in range(HALVES):
-                nc.vector.tensor_copy(x_got[o][s][:], x_tab[o][:].bitcast(U32).indirect(half_list(offs_t, s)))
+        def gather_x(o, s, tag):
+            got = keep.tile([P, HALF], U32, name="x_got%d%d" % (o, s), tag=tag, align_bytes=64)
+            nc.vector.tensor_copy(got[:], x_tab[o][:].bitcast(U32).indirect(half_list(offs_t, s)))
+            x_got[o, s] = got
 
         def quantise_h(b):
             grouped = keep.tile([P, PASSES, P * PACK], BF16, name="grouped%d" % b, tag="grouped%d" % b, align_bytes=64)
             for o in range(PASSES):
-                src = h_raw[b // 2][o][:, :, (b % 2) * P : (b % 2 + 1) * P]
                 nc.scalar.copy(
                     grouped[:, o, :].rearrange("p (c i j) -> p c j i", i=4, j=PACK),
-                    src.rearrange("p j (c i) -> p c j i", i=4),
+                    h_raw[b, o].rearrange("p j (c i) -> p c j i", i=4),
                 )
-            h_codes[b] = keep.tile([P, PASSES * P], U32, name="h_codes%d" % b, tag="xs_tab" if b == 0 else "h_codes%d" % b, align_bytes=64)
             nc.vector.quantize_mx(h_codes[b][:].bitcast(FP8X4), h_scales[b][:], grouped[:].rearrange("p o n -> p (o n)"))
 
         def one_pass(acc, b, o, codes, scales):
@@ -114,7 +129,7 @@ def tile_picked_yivf_sum_p_kernel(
             nc.scalar.copy(z_win[b][:, :R], acc[:])
 
         def y_pass(acc, b, s, o):
-            one_pass(acc[:], b, o, x_got[o][s][:], xs_got[4 * o : P, s * HALF : (s + 1) * HALF])
+            one_pass(acc[:], b, o, x_got[o, s][:], xs_mx[4 * o : P, s * HALF : (s + 1) * HALF])
 
         def store(b, s, res):
             nc.sync.dma_start(out=out[b * P : (b + 1) * P, s * HALF : (s + 1) * HALF], in_=res[:])
@@ -122,35 +137,47 @@ def tile_picked_yivf_sum_p_kernel(
         nc.vector.tensor_copy(es_got[:], es_tab[:].indirect(cent_t[:]))
         for o in range(PASSES):
             nc.vector.tensor_copy(e_got[o][:], e_tab[:, o, :].bitcast(U32).indirect(cent_t[:]))
-        nc.vector.tensor_copy(xs_got[:], xs_tab[:].indirect(offs_t[:]))
 
         z_got = {}
-        for b in range(EARLY):
-            quantise_h(b)
-            cell_scores(b, b % 2)
-            for s in range(HALVES):
-                z_got[b, s] = keep.tile([P, HALF], F32, name="z_got%d%d" % (b, s))
-                nc.vector.tensor_copy(z_got[b, s][:], z_win[b][:].indirect(half_list(cell_t, s)))
-        gather_x(0)
+
+        def gather_z(b, s, tag):
+            z_got[b, s] = keep.tile([P, HALF], F32, name="z_got%d%d" % (b, s), tag=tag, align_bytes=64)
+            nc.vector.tensor_copy(z_got[b, s][:], z_win[b][:].indirect(half_list(cell_t, s)))
+
+        quantise_h(0)
+        cell_scores(0, 0)
+        gather_z(0, 0, "z_got00")
+        quantise_h(1)
+        cell_scores(1, 1)
+        gather_z(0, 1, "grouped1")
+        gather_z(1, 0, "z_got10")
+        gather_z(1, 1, "z_got11")
+        gather_x(0, 0, "x_got00")
+        quantise_h(2)
+        cell_scores(2, 0)
+        gather_x(0, 1, "grouped2")
+        gather_z(2, 0, "z_got20")
+        gather_z(2, 1, "z_got21")
 
         y_acc = {}
         for s in range(HALVES):
             for b in range(EARLY):
                 y_acc[b, s] = psum.tile([P, HALF], F32, name="y%d%d" % (b, s), tag="bank%d" % (2 + 2 * b + s))
                 y_pass(y_acc[b, s], b, s, 0)
-        gather_x(1)
+        gather_x(1, 0, "x_got10")
+        gather_x(1, 1, "x_got11")
         for s in range(HALVES):
             for b in range(EARLY):
                 y_pass(y_acc[b, s], b, s, 1)
         for s in range(HALVES):
-            if s == 1:
-                quantise_h(EARLY)
             for b in range(EARLY):
-                res = keep.tile([P, HALF], F32, name="res%d%d" % (b, s), tag="grouped%d" % EARLY if (b, s) == (0, 1) else "res%d%d" % (b, s), align_bytes=64)
+                if (b, s) == (1, 0):
+                    quantise_h(EARLY)
+                res = keep.tile([P, HALF], F32, name="res%d%d" % (b, s), tag="grouped%d" % EARLY if (b, s) == (1, 0) else "res%d%d" % (b, s), align_bytes=64)
                 nc.vector.tensor_tensor(res[:], y_acc[b, s][:], z_got[b, s][:], ADD)
                 store(b, s, res)
 
-        late_banks = {2: (6, 0, 1), 3: (7, 6, 2)}
+        late_banks = {3: (1, 0, 2)}
         for b in range(EARLY, BLOCKS):
             if b > EARLY:
                 quantise_h(b)

@@ -21,8 +21,6 @@ BLOCKS = 4
 HALF = 512
 HALVES = 2
 Z_WINDOW = 544
-EARLY = 3
-H_LOADS = [(0, 1), (1, 2), (2, 3), (3, 4)]
 
 
 def tile_picked_yivf_sum_p_kernel(
@@ -36,31 +34,28 @@ def tile_picked_yivf_sum_p_kernel(
         offs_t = keep.tile([P, S // 16], U16, name="offs_t")
         cent_t = keep.tile([P, R // 16], U16, name="cent_t")
         cell_t = keep.tile([P, S // 16], U16, name="cell_t")
-        x_tab = [keep.tile([P, T], I32, name="x_tab%d" % o, align_bytes=64) for o in range(PASSES)]
-        e_tab = keep.tile([P, PASSES, W], I32, name="e_tab", align_bytes=64)
+        x_tab = [keep.tile([P, T], I32, name="x_tab%d" % o, tag="x_tab%d" % o, align_bytes=64) for o in range(PASSES)]
+        e_tab = [keep.tile([P, W], I32, name="e_tab%d" % o, align_bytes=64) for o in range(PASSES)]
         xs_tab = keep.tile([P, T], U8, name="xs_tab", align_bytes=64)
         es_tab = keep.tile([P, W], U8, name="es_tab", align_bytes=64)
         xs_got = keep.tile([P, S], U8, name="xs_got", align_bytes=64)
-        xs_mx = keep.tile([P, S], U8, name="xs_mx", align_bytes=64)
+        xs_mx = [keep.tile([P, S], U8, name="xs_mx%d" % o, align_bytes=64) for o in range(PASSES)]
         z_win = [keep.tile([P, Z_WINDOW], F32, name="z_win%d" % b, align_bytes=64) for b in range(BLOCKS)]
 
         nc.gpsimd.memset(es_tab[:].bitcast(I32), 0)
         nc.vector.memset(xs_tab[32:64, :].bitcast(I32), 0)
         nc.vector.memset(xs_tab[64:128, :].bitcast(I32), 0)
-        nc.gpsimd.memset(xs_mx[:].bitcast(I32), 0)
+        for o in range(PASSES):
+            nc.gpsimd.memset(xs_mx[o][:].bitcast(I32), 0)
         for b in range(BLOCKS):
             nc.gpsimd.memset(z_win[b][:, R:], 0.0)
 
         h_raw = {}
 
-        def load_h(g):
-            first, last = H_LOADS[g]
-            for o in range(PASSES):
-                raw = keep.tile([P, PACK, (last - first) * P], F32, name="h_raw%d%d" % (g, o), align_bytes=64)
-                rows = hT[512 * o : 512 * (o + 1), first * P : last * P]
-                nc.sync.dma_start(out=raw[:], in_=rows.rearrange("(p j) c -> p j c", j=PACK))
-                for b in range(first, last):
-                    h_raw[b, o] = raw[:, :, (b - first) * P : (b - first + 1) * P]
+        def load_h(o):
+            raw = keep.tile([P, PACK, V], F32, name="h_raw%d" % o, align_bytes=64)
+            nc.sync.dma_start(out=raw[:], in_=hT[512 * o : 512 * (o + 1), :].rearrange("(p j) c -> p j c", j=PACK))
+            h_raw[o] = raw
 
         def load_x(o):
             nc.sync.dma_start(out=x_tab[o][:], in_=x_words[o].rearrange("p n t -> p (n t)").bitcast(I32))
@@ -68,31 +63,29 @@ def tile_picked_yivf_sum_p_kernel(
         def place_x_scales(o):
             for q in range(4):
                 src = 16 * o + 4 * q
-                dst = 32 * q + 4 * o
-                nc.sync.dma_start(out=xs_mx[dst : dst + 4, :].bitcast(I32), in_=xs_got[src : src + 4, :].bitcast(I32))
+                dst = 32 * q
+                nc.sync.dma_start(out=xs_mx[o][dst : dst + 4, :].bitcast(I32), in_=xs_got[src : src + 4, :].bitcast(I32))
 
         nc.sync.dma_start(offs_t[:], offs)
         nc.sync.dma_start(out=xs_tab[0:32, :].bitcast(I32), in_=x_scales.rearrange("o q c -> (o q) c").bitcast(I32))
         nc.sync.dma_start(cent_t[:], cent)
-        for q in range(4):
-            nc.scalar.dma_start(out=es_tab[32 * q : 32 * q + 8, :].bitcast(I32), in_=e_scales[:, 4 * q : 4 * q + 4, :].bitcast(I32))
-        nc.sync.dma_start(out=e_tab[:], in_=e_words.rearrange("o p n t -> p o (n t)").bitcast(I32))
-        nc.vector.tensor_copy(xs_got[:], xs_tab[:].indirect(offs_t[:]))
         load_h(0)
+        for q in range(4):
+            nc.sync.dma_start(out=es_tab[32 * q : 32 * q + 8, :].bitcast(I32), in_=e_scales[:, 4 * q : 4 * q + 4, :].bitcast(I32))
         load_h(1)
+        for o in range(PASSES):
+            nc.sync.dma_start(out=e_tab[o][:], in_=e_words[o].rearrange("p n t -> p (n t)").bitcast(I32))
+        nc.vector.tensor_copy(xs_got[:], xs_tab[:].indirect(offs_t[:]))
         nc.sync.dma_start(cell_t[:], cell)
         load_x(0)
         place_x_scales(0)
-        load_h(2)
         load_x(1)
         place_x_scales(1)
-        load_h(3)
 
         es_got = keep.tile([P, R], U8, name="es_got", align_bytes=64)
         e_got = [keep.tile([P, R], U32, name="e_got%d" % o, align_bytes=64) for o in range(PASSES)]
         x_got = {}
-        h_codes = [keep.tile([P, PASSES * P], U32, name="h_codes%d" % b, align_bytes=64) for b in range(BLOCKS)]
-        h_scales = [keep.tile([P, PASSES * P], U8, name="h_scales%d" % b, align_bytes=64) for b in range(BLOCKS)]
+        h_mx = {}
 
         def half_list(t, s):
             return t[:, s * HALF // 16 : (s + 1) * HALF // 16]
@@ -102,20 +95,23 @@ def tile_picked_yivf_sum_p_kernel(
             nc.vector.tensor_copy(got[:], x_tab[o][:].bitcast(U32).indirect(half_list(offs_t, s)))
             x_got[o, s] = got
 
-        def quantise_h(b):
-            grouped = keep.tile([P, PASSES, P * PACK], BF16, name="grouped%d" % b, tag="grouped%d" % b, align_bytes=64)
-            for o in range(PASSES):
-                nc.scalar.copy(
-                    grouped[:, o, :].rearrange("p (c i j) -> p c j i", i=4, j=PACK),
-                    h_raw[b, o].rearrange("p j (c i) -> p c j i", i=4),
-                )
-            nc.vector.quantize_mx(h_codes[b][:].bitcast(FP8X4), h_scales[b][:], grouped[:].rearrange("p o n -> p (o n)"))
+        def quantise_h(o, g):
+            grouped = keep.tile([P, 2 * P * PACK], BF16, name="grouped%d%d" % (o, g), align_bytes=64)
+            cast = nc.vector.tensor_copy if (o, g) == (1, 1) else nc.scalar.copy
+            cast(
+                grouped[:].rearrange("p (c i j) -> p c j i", i=4, j=PACK),
+                h_raw[o][:, :, 2 * P * g : 2 * P * (g + 1)].rearrange("p j (c i) -> p c j i", i=4),
+            )
+            codes = keep.tile([P, 2 * P], U32, name="h_codes%d%d" % (o, g), align_bytes=64)
+            scales = keep.tile([P, 2 * P], U8, name="h_scales%d%d" % (o, g), align_bytes=64)
+            nc.vector.quantize_mx(codes[:].bitcast(FP8X4), scales[:], grouped[:])
+            h_mx[o, g] = (codes, scales)
 
         def one_pass(acc, b, o, codes, scales):
             nc.tensor.matmul_mx(
                 acc,
-                lhsT=h_codes[b][:, o * P : (o + 1) * P].bitcast(FP8X4),
-                lhsT_scale=h_scales[b][:, o * P : (o + 1) * P],
+                lhsT=h_mx[o, b // 2][0][:, b % 2 * P : (b % 2 + 1) * P].bitcast(FP8X4),
+                lhsT_scale=h_mx[o, b // 2][1][:, b % 2 * P : (b % 2 + 1) * P],
                 rhs=codes.bitcast(FP8X4),
                 rhs_scale=scales,
                 start=(o == 0),
@@ -129,14 +125,11 @@ def tile_picked_yivf_sum_p_kernel(
             nc.scalar.copy(z_win[b][:, :R], acc[:])
 
         def y_pass(acc, b, s, o):
-            one_pass(acc[:], b, o, x_got[o, s][:], xs_mx[4 * o : P, s * HALF : (s + 1) * HALF])
+            one_pass(acc[:], b, o, x_got[o, s][:], xs_mx[o][:, s * HALF : (s + 1) * HALF])
 
-        def store(b, s, res):
-            nc.sync.dma_start(out=out[b * P : (b + 1) * P, s * HALF : (s + 1) * HALF], in_=res[:])
+        def store(b, first, res):
+            nc.sync.dma_start(out=out[b * P : (b + 1) * P, first : first + res.shape[1]], in_=res[:])
 
-        nc.vector.tensor_copy(es_got[:], es_tab[:].indirect(cent_t[:]))
-        for o in range(PASSES):
-            nc.vector.tensor_copy(e_got[o][:], e_tab[:, o, :].bitcast(U32).indirect(cent_t[:]))
 
         z_got = {}
 
@@ -144,50 +137,43 @@ def tile_picked_yivf_sum_p_kernel(
             z_got[b, s] = keep.tile([P, HALF], F32, name="z_got%d%d" % (b, s), tag=tag, align_bytes=64)
             nc.vector.tensor_copy(z_got[b, s][:], z_win[b][:].indirect(half_list(cell_t, s)))
 
-        quantise_h(0)
-        cell_scores(0, 0)
-        gather_z(0, 0, "z_got00")
-        quantise_h(1)
-        cell_scores(1, 1)
-        gather_z(0, 1, "grouped1")
-        gather_z(1, 0, "z_got10")
-        gather_z(1, 1, "z_got11")
-        gather_x(0, 0, "x_got00")
-        quantise_h(2)
-        cell_scores(2, 0)
-        gather_x(0, 1, "grouped2")
-        gather_z(2, 0, "z_got20")
-        gather_z(2, 1, "z_got21")
+        for g in range(2):
+            quantise_h(0, g)
+        nc.vector.tensor_copy(es_got[:], es_tab[:].indirect(cent_t[:]))
+        for g in range(2):
+            quantise_h(1, g)
+        for o in range(PASSES):
+            nc.vector.tensor_copy(e_got[o][:], e_tab[o][:].bitcast(U32).indirect(cent_t[:]))
+        for b in range(BLOCKS):
+            cell_scores(b, b % 2)
+        early = [(0, 0), (1, 0), (0, 1)]
+        for b, s in early[:2]:
+            gather_z(b, s, "z_got%d%d" % (b, s))
 
         y_acc = {}
-        for s in range(HALVES):
-            for b in range(EARLY):
-                y_acc[b, s] = psum.tile([P, HALF], F32, name="y%d%d" % (b, s), tag="bank%d" % (2 + 2 * b + s))
-                y_pass(y_acc[b, s], b, s, 0)
-        gather_x(1, 0, "x_got10")
-        gather_x(1, 1, "x_got11")
-        for s in range(HALVES):
-            for b in range(EARLY):
-                y_pass(y_acc[b, s], b, s, 1)
-        for s in range(HALVES):
-            for b in range(EARLY):
-                if (b, s) == (1, 0):
-                    quantise_h(EARLY)
-                res = keep.tile([P, HALF], F32, name="res%d%d" % (b, s), tag="grouped%d" % EARLY if (b, s) == (1, 0) else "res%d%d" % (b, s), align_bytes=64)
-                nc.vector.tensor_tensor(res[:], y_acc[b, s][:], z_got[b, s][:], ADD)
-                store(b, s, res)
-
-        late_banks = {3: (1, 0, 2)}
-        for b in range(EARLY, BLOCKS):
-            if b > EARLY:
-                quantise_h(b)
-            cell_scores(b, late_banks[b][0])
+        for o in range(PASSES):
             for s in range(HALVES):
-                acc = psum.tile([P, HALF], F32, name="y%d%d" % (b, s), tag="bank%d" % late_banks[b][1 + s])
-                for o in range(PASSES):
-                    y_pass(acc, b, s, o)
-                y_sb = keep.tile([P, HALF], F32, name="y_sb%d%d" % (b, s))
-                nc.scalar.copy(y_sb[:], acc[:])
-                res = keep.tile([P, HALF], F32, name="res%d%d" % (b, s))
-                nc.vector.tensor_tensor(res[:], z_win[b][:].indirect(half_list(cell_t, s)), y_sb[:], ADD)
-                store(b, s, res)
+                gather_x(o, s, "x_got%d%d" % (o, s))
+                for b in range(BLOCKS):
+                    if o == 0:
+                        y_acc[b, s] = psum.tile([P, HALF], F32, name="y%d%d" % (b, s), tag="bank%d" % (BLOCKS * s + b))
+                    y_pass(y_acc[b, s], b, s, o)
+            if o == 0:
+                gather_z(0, 1, "x_tab0")
+
+        for s in range(HALVES):
+            for b in range(BLOCKS):
+                if (b, s) in early:
+                    res = keep.tile([P, HALF], F32, name="res%d%d" % (b, s), align_bytes=64)
+                    nc.vector.tensor_tensor(res[:], y_acc[b, s][:], z_got[b, s][:], ADD)
+                    store(b, s * HALF, res)
+                else:
+                    y_sb = keep.tile([P, HALF], F32, name="y_sb%d%d" % (b, s))
+                    nc.scalar.copy(y_sb[:], y_acc[b, s][:])
+                    width = HALF // 2 if (b, s) == (BLOCKS - 1, HALVES - 1) else HALF
+                    for c in range(0, HALF, width):
+                        first = s * HALF + c
+                        res = keep.tile([P, width], F32, name="res%d_%d" % (b, first), align_bytes=64)
+                        cells = cell_t[:, first // 16 : (first + width) // 16]
+                        nc.vector.tensor_tensor(res[:], z_win[b][:].indirect(cells), y_sb[:, c : c + width], ADD)
+                        store(b, first, res)

@@ -40,25 +40,32 @@ def tile_picked_yivf_sum_p_kernel(
         es_tab = keep.tile([P, W], U8, name="es_tab", align_bytes=64)
         xs_got = keep.tile([P, S], U8, name="xs_got", align_bytes=64)
         xs_mx = [keep.tile([P, S], U8, name="xs_mx%d" % o, align_bytes=64) for o in range(PASSES)]
-        z_win = [keep.tile([P, Z_WINDOW], F32, name="z_win%d" % b, align_bytes=64) for b in range(BLOCKS)]
+        z_win = [keep.tile([P, Z_WINDOW], F32, name="z_win%d" % b, tag="z_win%d" % b, align_bytes=64) for b in range(BLOCKS)]
 
         nc.gpsimd.memset(es_tab[:].bitcast(I32), 0)
-        nc.vector.memset(xs_tab[32:64, :].bitcast(I32), 0)
+        nc.gpsimd.memset(xs_tab[32:64, :].bitcast(I32), 0)
         nc.vector.memset(xs_tab[64:128, :].bitcast(I32), 0)
         for o in range(PASSES):
             nc.gpsimd.memset(xs_mx[o][:].bitcast(I32), 0)
         for b in range(BLOCKS):
             nc.gpsimd.memset(z_win[b][:, R:], 0.0)
 
+        groups = [(b, 1) for b in range(BLOCKS)]
         h_raw = {}
 
-        def load_h(o):
-            raw = keep.tile([P, PACK, V], F32, name="h_raw%d" % o, align_bytes=64)
-            nc.sync.dma_start(out=raw[:], in_=hT[512 * o : 512 * (o + 1), :].rearrange("(p j) c -> p j c", j=PACK))
-            h_raw[o] = raw
+        def load_h(g):
+            first, count = groups[g]
+            for o in range(PASSES):
+                raw = keep.tile([P, PACK, count * P], F32, name="h_raw%d%d" % (o, g), align_bytes=64)
+                rows = hT[512 * o : 512 * (o + 1), P * first : P * (first + count)]
+                nc.sync.dma_start(out=raw[:], in_=rows.rearrange("(p j) c -> p j c", j=PACK))
+                h_raw[o, g] = raw
 
         def load_x(o):
             nc.sync.dma_start(out=x_tab[o][:], in_=x_words[o].rearrange("p n t -> p (n t)").bitcast(I32))
+
+        def load_e(o):
+            nc.sync.dma_start(out=e_tab[o][:], in_=e_words[o].rearrange("p n t -> p (n t)").bitcast(I32))
 
         def place_x_scales(o):
             for q in range(4):
@@ -68,19 +75,20 @@ def tile_picked_yivf_sum_p_kernel(
 
         nc.sync.dma_start(offs_t[:], offs)
         nc.sync.dma_start(out=xs_tab[0:32, :].bitcast(I32), in_=x_scales.rearrange("o q c -> (o q) c").bitcast(I32))
-        nc.sync.dma_start(cent_t[:], cent)
         load_h(0)
+        load_e(0)
         for q in range(4):
             nc.sync.dma_start(out=es_tab[32 * q : 32 * q + 8, :].bitcast(I32), in_=e_scales[:, 4 * q : 4 * q + 4, :].bitcast(I32))
+        nc.sync.dma_start(cent_t[:], cent)
+        load_e(1)
         load_h(1)
-        for o in range(PASSES):
-            nc.sync.dma_start(out=e_tab[o][:], in_=e_words[o].rearrange("p n t -> p (n t)").bitcast(I32))
-        nc.vector.tensor_copy(xs_got[:], xs_tab[:].indirect(offs_t[:]))
         nc.sync.dma_start(cell_t[:], cell)
-        load_x(0)
-        place_x_scales(0)
-        load_x(1)
-        place_x_scales(1)
+        load_h(2)
+        nc.vector.tensor_copy(xs_got[:], xs_tab[:].indirect(offs_t[:]))
+        for o in range(PASSES):
+            place_x_scales(o)
+            load_x(o)
+        load_h(3)
 
         es_got = keep.tile([P, R], U8, name="es_got", align_bytes=64)
         e_got = [keep.tile([P, R], U32, name="e_got%d" % o, align_bytes=64) for o in range(PASSES)]
@@ -90,90 +98,115 @@ def tile_picked_yivf_sum_p_kernel(
         def half_list(t, s):
             return t[:, s * HALF // 16 : (s + 1) * HALF // 16]
 
-        def gather_x(o, s, tag):
-            got = keep.tile([P, HALF], U32, name="x_got%d%d" % (o, s), tag=tag, align_bytes=64)
+        def gather_x(o, s):
+            got = keep.tile([P, HALF], U32, name="x_got%d%d" % (o, s), align_bytes=64)
             nc.vector.tensor_copy(got[:], x_tab[o][:].bitcast(U32).indirect(half_list(offs_t, s)))
             x_got[o, s] = got
 
-        def quantise_h(o, g):
-            grouped = keep.tile([P, 2 * P * PACK], BF16, name="grouped%d%d" % (o, g), align_bytes=64)
-            cast = nc.vector.tensor_copy if (o, g) == (1, 1) else nc.scalar.copy
-            cast(
-                grouped[:].rearrange("p (c i j) -> p c j i", i=4, j=PACK),
-                h_raw[o][:, :, 2 * P * g : 2 * P * (g + 1)].rearrange("p j (c i) -> p c j i", i=4),
-            )
-            codes = keep.tile([P, 2 * P], U32, name="h_codes%d%d" % (o, g), align_bytes=64)
-            scales = keep.tile([P, 2 * P], U8, name="h_scales%d%d" % (o, g), align_bytes=64)
-            nc.vector.quantize_mx(codes[:].bitcast(FP8X4), scales[:], grouped[:])
-            h_mx[o, g] = (codes, scales)
+        def quantise_h(g, tag):
+            first, count = groups[g]
+            both = keep.tile([P, PASSES * count * P * PACK], BF16, name="grouped%d" % g, tag=tag, align_bytes=64)
+            for o in range(PASSES):
+                grouped = both[:, o * count * P * PACK : (o + 1) * count * P * PACK]
+                nc.scalar.copy(
+                    grouped.rearrange("p (c i j) -> p c j i", i=4, j=PACK),
+                    h_raw[o, g][:].rearrange("p j (c i) -> p c j i", i=4),
+                )
+                codes = keep.tile([P, count * P], U32, name="h_codes%d%d" % (o, g), align_bytes=64)
+                scales = keep.tile([P, count * P], U8, name="h_scales%d%d" % (o, g), align_bytes=64)
+                nc.vector.quantize_mx(codes[:].bitcast(FP8X4), scales[:], grouped)
+                for i in range(count):
+                    h_mx[o, first + i] = (codes[:, i * P : (i + 1) * P], scales[:, i * P : (i + 1) * P])
 
         def one_pass(acc, b, o, codes, scales):
             nc.tensor.matmul_mx(
                 acc,
-                lhsT=h_mx[o, b // 2][0][:, b % 2 * P : (b % 2 + 1) * P].bitcast(FP8X4),
-                lhsT_scale=h_mx[o, b // 2][1][:, b % 2 * P : (b % 2 + 1) * P],
+                lhsT=h_mx[o, b][0].bitcast(FP8X4),
+                lhsT_scale=h_mx[o, b][1],
                 rhs=codes.bitcast(FP8X4),
                 rhs_scale=scales,
                 start=(o == 0),
                 stop=(o == PASSES - 1),
             )
 
-        def cell_scores(b, bank):
-            acc = psum.tile([P, R], F32, name="z%d" % b, tag="bank%d" % bank)
+        def cell_scores(b):
+            acc = psum.tile([P, R], F32, name="z%d" % b, tag="bank%d" % (7 if b == 1 else 6))
             for o in range(PASSES):
                 one_pass(acc[:], b, o, e_got[o][:], es_got[4 * o : P, :])
             nc.scalar.copy(z_win[b][:, :R], acc[:])
 
-        def y_pass(acc, b, s, o):
-            one_pass(acc[:], b, o, x_got[o, s][:], xs_mx[o][:, s * HALF : (s + 1) * HALF])
-
         def store(b, first, res):
             nc.sync.dma_start(out=out[b * P : (b + 1) * P, first : first + res.shape[1]], in_=res[:])
 
-
         z_got = {}
 
-        def gather_z(b, s, tag):
-            z_got[b, s] = keep.tile([P, HALF], F32, name="z_got%d%d" % (b, s), tag=tag, align_bytes=64)
-            nc.vector.tensor_copy(z_got[b, s][:], z_win[b][:].indirect(half_list(cell_t, s)))
-
-        for g in range(2):
-            quantise_h(0, g)
-        nc.vector.tensor_copy(es_got[:], es_tab[:].indirect(cent_t[:]))
-        for g in range(2):
-            quantise_h(1, g)
-        for o in range(PASSES):
-            nc.vector.tensor_copy(e_got[o][:], e_tab[o][:].bitcast(U32).indirect(cent_t[:]))
-        for b in range(BLOCKS):
-            cell_scores(b, b % 2)
-        early = [(0, 0), (1, 0), (0, 1)]
-        for b, s in early[:2]:
-            gather_z(b, s, "z_got%d%d" % (b, s))
+        def gather_z(b, s, dst):
+            nc.vector.tensor_copy(dst, z_win[b][:].indirect(half_list(cell_t, s)))
+            z_got[b, s] = dst
 
         y_acc = {}
-        for o in range(PASSES):
-            for s in range(HALVES):
-                gather_x(o, s, "x_got%d%d" % (o, s))
-                for b in range(BLOCKS):
-                    if o == 0:
-                        y_acc[b, s] = psum.tile([P, HALF], F32, name="y%d%d" % (b, s), tag="bank%d" % (BLOCKS * s + b))
-                    y_pass(y_acc[b, s], b, s, o)
-            if o == 0:
-                gather_z(0, 1, "x_tab0")
 
+        def scan_pass(o):
+            for s in range(HALVES):
+                gather_x(o, s)
+                for b in range(3):
+                    if o == 0:
+                        y_acc[b, s] = psum.tile([P, HALF], F32, name="y%d%d" % (b, s), tag="bank%d" % (3 * s + b))
+                    one_pass(y_acc[b, s][:], b, o, x_got[o, s][:], xs_mx[o][:, s * HALF : (s + 1) * HALF])
+
+        quantise_h(0, "grouped0")
+        nc.vector.tensor_copy(e_got[0][:], e_tab[0][:].bitcast(U32).indirect(cent_t[:]))
+        nc.vector.tensor_copy(es_got[:], es_tab[:].indirect(cent_t[:]))
+        nc.vector.tensor_copy(e_got[1][:], e_tab[1][:].bitcast(U32).indirect(cent_t[:]))
+        quantise_h(1, "grouped1")
+        for b in range(2):
+            cell_scores(b)
+            for s in range(HALVES):
+                tag = "grouped1" if (b, s) == (0, 1) else "z_got%d%d" % (b, s)
+                early = keep.tile([P, HALF], F32, name="z_got%d%d" % (b, s), tag=tag, align_bytes=64)
+                gather_z(b, s, early[:])
+        quantise_h(2, "z_win0")
+        cell_scores(2)
+        scan_pass(0)
+        between = keep.tile([P, HALF], F32, name="between", tag="x_tab0", align_bytes=64)
+        gather_z(2, 0, between[:])
+        scan_pass(1)
+        quantise_h(3, "grouped3")
+
+        def copy_out(b, s):
+            y_sb = keep.tile([P, HALF], F32, name="y_sb%d%d" % (b, s))
+            nc.scalar.copy(y_sb[:], y_acc[b, s][:])
+            return y_sb
+
+        def sum_on_vector(b, s):
+            res = keep.tile([P, HALF], F32, name="res%d%d" % (b, s), align_bytes=64)
+            nc.vector.tensor_tensor(res[:], y_acc[b, s][:], z_got[b, s], ADD)
+            store(b, s * HALF, res)
+
+        def sum_on_gpsimd(b, s, queue):
+            y_sb = copy_out(b, s)
+            res = keep.tile([P, HALF], F32, name="res%d%d" % (b, s), align_bytes=64)
+            nc.gpsimd.tensor_tensor(res[:], y_sb[:], z_got[b, s], ADD)
+            queue.dma_start(out=out[b * P : (b + 1) * P, s * HALF : (s + 1) * HALF], in_=res[:])
+
+        def gather_and_sum(b, s, width):
+            y_sb = copy_out(b, s)
+            for c in range(0, HALF, width):
+                first = s * HALF + c
+                res = keep.tile([P, width], F32, name="res%d_%d" % (b, first), align_bytes=64)
+                cells = cell_t[:, first // 16 : (first + width) // 16]
+                nc.vector.tensor_tensor(res[:], z_win[b][:].indirect(cells), y_sb[:, c : c + width], ADD)
+                store(b, first, res)
+
+        sum_on_gpsimd(0, 0, nc.sync)
+        sum_on_gpsimd(1, 0, nc.sync)
+        sum_on_vector(2, 0)
+        sum_on_vector(0, 1)
+        sum_on_vector(1, 1)
+        gather_and_sum(2, 1, HALF)
+        cell_scores(3)
         for s in range(HALVES):
-            for b in range(BLOCKS):
-                if (b, s) in early:
-                    res = keep.tile([P, HALF], F32, name="res%d%d" % (b, s), align_bytes=64)
-                    nc.vector.tensor_tensor(res[:], y_acc[b, s][:], z_got[b, s][:], ADD)
-                    store(b, s * HALF, res)
-                else:
-                    y_sb = keep.tile([P, HALF], F32, name="y_sb%d%d" % (b, s))
-                    nc.scalar.copy(y_sb[:], y_acc[b, s][:])
-                    width = HALF // 2 if (b, s) == (BLOCKS - 1, HALVES - 1) else HALF
-                    for c in range(0, HALF, width):
-                        first = s * HALF + c
-                        res = keep.tile([P, width], F32, name="res%d_%d" % (b, first), align_bytes=64)
-                        cells = cell_t[:, first // 16 : (first + width) // 16]
-                        nc.vector.tensor_tensor(res[:], z_win[b][:].indirect(cells), y_sb[:, c : c + width], ADD)
-                        store(b, first, res)
+            y_acc[3, s] = psum.tile([P, HALF], F32, name="y3%d" % s, tag="bank%d" % (7 if s == 0 else 0))
+            for o in range(PASSES):
+                one_pass(y_acc[3, s][:], 3, o, x_got[o, s][:], xs_mx[o][:, s * HALF : (s + 1) * HALF])
+            gather_and_sum(3, s, HALF if s == 0 else 256)

@@ -38,7 +38,7 @@ def tile_picked_yivf_sum_p_kernel(
         e_tab = [keep.tile([P, W], I32, name="e_tab%d" % o, align_bytes=64) for o in range(PASSES)]
         xs_tab = keep.tile([P, T], U8, name="xs_tab", align_bytes=64)
         es_tab = keep.tile([P, W], U8, name="es_tab", align_bytes=64)
-        xs_got = keep.tile([P, S], U8, name="xs_got", align_bytes=64)
+        xs_got = keep.tile([P, S], U8, name="xs_got", tag="xs_got", align_bytes=64)
         xs_mx = [keep.tile([P, S], U8, name="xs_mx%d" % o, align_bytes=64) for o in range(PASSES)]
         z_win = [keep.tile([P, Z_WINDOW], F32, name="z_win%d" % b, tag="z_win%d" % b, align_bytes=64) for b in range(BLOCKS)]
 
@@ -56,7 +56,7 @@ def tile_picked_yivf_sum_p_kernel(
         def load_h(g):
             first, count = groups[g]
             for o in range(PASSES):
-                raw = keep.tile([P, PACK, count * P], F32, name="h_raw%d%d" % (o, g), align_bytes=64)
+                raw = keep.tile([P, PACK, count * P], F32, name="h_raw%d%d" % (o, g), tag="h_raw%d%d" % (o, g), align_bytes=64)
                 rows = hT[512 * o : 512 * (o + 1), P * first : P * (first + count)]
                 nc.sync.dma_start(out=raw[:], in_=rows.rearrange("(p j) c -> p j c", j=PACK))
                 h_raw[o, g] = raw
@@ -67,8 +67,9 @@ def tile_picked_yivf_sum_p_kernel(
         def load_e(o):
             nc.sync.dma_start(out=e_tab[o][:], in_=e_words[o].rearrange("p n t -> p (n t)").bitcast(I32))
 
-        def place_x_scales(o):
-            for q in range(4):
+        def place_x_scales(first, last):
+            for i in range(first, last):
+                o, q = divmod(i, 4)
                 src = 16 * o + 4 * q
                 dst = 32 * q
                 nc.sync.dma_start(out=xs_mx[o][dst : dst + 4, :].bitcast(I32), in_=xs_got[src : src + 4, :].bitcast(I32))
@@ -85,9 +86,10 @@ def tile_picked_yivf_sum_p_kernel(
         nc.sync.dma_start(cell_t[:], cell)
         load_h(2)
         nc.vector.tensor_copy(xs_got[:], xs_tab[:].indirect(offs_t[:]))
-        for o in range(PASSES):
-            place_x_scales(o)
-            load_x(o)
+        place_x_scales(0, 2)
+        load_x(0)
+        place_x_scales(2, 8)
+        load_x(1)
         load_h(3)
 
         es_got = keep.tile([P, R], U8, name="es_got", align_bytes=64)
@@ -162,35 +164,35 @@ def tile_picked_yivf_sum_p_kernel(
         for b in range(2):
             cell_scores(b)
             for s in range(HALVES):
-                tag = "grouped1" if (b, s) == (0, 1) else "z_got%d%d" % (b, s)
+                tag = "h_raw11" if (b, s) == (0, 1) else "z_got%d%d" % (b, s)
                 early = keep.tile([P, HALF], F32, name="z_got%d%d" % (b, s), tag=tag, align_bytes=64)
                 gather_z(b, s, early[:])
         quantise_h(2, "z_win0")
         cell_scores(2)
         scan_pass(0)
-        between = keep.tile([P, HALF], F32, name="between", tag="x_tab0", align_bytes=64)
+        between = keep.tile([P, HALF], F32, name="between", tag="xs_got", align_bytes=64)
         gather_z(2, 0, between[:])
         scan_pass(1)
         quantise_h(3, "grouped3")
 
-        def copy_out(b, s):
-            y_sb = keep.tile([P, HALF], F32, name="y_sb%d%d" % (b, s))
-            nc.scalar.copy(y_sb[:], y_acc[b, s][:])
+        def copy_out(b, s, c, width):
+            y_sb = keep.tile([P, width], F32, name="y_sb%d%d" % (b, s), align_bytes=64)
+            nc.scalar.copy(y_sb[:], y_acc[b, s][:, c : c + width])
             return y_sb
 
-        def sum_on_vector(b, s):
-            res = keep.tile([P, HALF], F32, name="res%d%d" % (b, s), align_bytes=64)
-            nc.vector.tensor_tensor(res[:], y_acc[b, s][:], z_got[b, s], ADD)
-            store(b, s * HALF, res)
+        def sum_on_vector(b, s, c, width):
+            res = keep.tile([P, width], F32, name="res%d_%d" % (b, s * HALF + c), align_bytes=64)
+            nc.vector.tensor_tensor(res[:], y_acc[b, s][:, c : c + width], z_got[b, s][:, c : c + width], ADD)
+            store(b, s * HALF + c, res)
 
-        def sum_on_gpsimd(b, s, queue):
-            y_sb = copy_out(b, s)
-            res = keep.tile([P, HALF], F32, name="res%d%d" % (b, s), align_bytes=64)
-            nc.gpsimd.tensor_tensor(res[:], y_sb[:], z_got[b, s], ADD)
-            queue.dma_start(out=out[b * P : (b + 1) * P, s * HALF : (s + 1) * HALF], in_=res[:])
+        def sum_on_gpsimd(b, s, c, width):
+            y_sb = copy_out(b, s, c, width)
+            res = keep.tile([P, width], F32, name="res%d_%d" % (b, s * HALF + c), align_bytes=64)
+            nc.gpsimd.tensor_tensor(res[:], y_sb[:], z_got[b, s][:, c : c + width], ADD)
+            store(b, s * HALF + c, res)
 
         def gather_and_sum(b, s, width):
-            y_sb = copy_out(b, s)
+            y_sb = copy_out(b, s, 0, HALF)
             for c in range(0, HALF, width):
                 first = s * HALF + c
                 res = keep.tile([P, width], F32, name="res%d_%d" % (b, first), align_bytes=64)
@@ -198,11 +200,12 @@ def tile_picked_yivf_sum_p_kernel(
                 nc.vector.tensor_tensor(res[:], z_win[b][:].indirect(cells), y_sb[:, c : c + width], ADD)
                 store(b, first, res)
 
-        sum_on_gpsimd(0, 0, nc.sync)
-        sum_on_gpsimd(1, 0, nc.sync)
-        sum_on_vector(2, 0)
-        sum_on_vector(0, 1)
-        sum_on_vector(1, 1)
+        sum_on_gpsimd(0, 0, 0, HALF)
+        sum_on_vector(1, 0, HALF // 2, HALF // 2)
+        sum_on_gpsimd(1, 0, 0, HALF // 2)
+        sum_on_vector(2, 0, 0, HALF)
+        sum_on_vector(0, 1, 0, HALF)
+        sum_on_vector(1, 1, 0, HALF)
         gather_and_sum(2, 1, HALF)
         cell_scores(3)
         for s in range(HALVES):

@@ -13,14 +13,17 @@ U16 = mybir.dt.uint16
 U8 = mybir.dt.uint8
 FP8X4 = mybir.dt.float8_e4m3fn_x4
 ADD = mybir.AluOpType.add
+COPY = mybir.ActivationFunctionType.Copy
 
 P = 128
 PACK = 4
 PASSES = 2
 BLOCKS = 4
+EARLY = 3
 HALF = 512
 HALVES = 2
 Z_WINDOW = 544
+X_SPLIT = 3072
 
 
 def tile_picked_yivf_sum_p_kernel(
@@ -34,13 +37,13 @@ def tile_picked_yivf_sum_p_kernel(
         offs_t = keep.tile([P, S // 16], U16, name="offs_t")
         cent_t = keep.tile([P, R // 16], U16, name="cent_t")
         cell_t = keep.tile([P, S // 16], U16, name="cell_t")
-        x_tab = [keep.tile([P, T], I32, name="x_tab%d" % o, tag="x_tab%d" % o, align_bytes=64) for o in range(PASSES)]
+        x_tab = [keep.tile([P, T], I32, name="x_tab%d" % o, align_bytes=64) for o in range(PASSES)]
         e_tab = [keep.tile([P, W], I32, name="e_tab%d" % o, align_bytes=64) for o in range(PASSES)]
         xs_tab = keep.tile([P, T], U8, name="xs_tab", align_bytes=64)
         es_tab = keep.tile([P, W], U8, name="es_tab", align_bytes=64)
-        xs_got = keep.tile([P, S], U8, name="xs_got", tag="xs_got", align_bytes=64)
+        xs_got = keep.tile([P, S], U8, name="xs_got", align_bytes=64)
         xs_mx = [keep.tile([P, S], U8, name="xs_mx%d" % o, align_bytes=64) for o in range(PASSES)]
-        z_win = [keep.tile([P, Z_WINDOW], F32, name="z_win%d" % b, tag="z_win%d" % b, align_bytes=64) for b in range(BLOCKS)]
+        z_win = [keep.tile([P, Z_WINDOW], F32, name="z_win%d" % b, align_bytes=64) for b in range(BLOCKS)]
 
         nc.gpsimd.memset(es_tab[:].bitcast(I32), 0)
         nc.gpsimd.memset(xs_tab[32:64, :].bitcast(I32), 0)
@@ -50,47 +53,55 @@ def tile_picked_yivf_sum_p_kernel(
         for b in range(BLOCKS):
             nc.gpsimd.memset(z_win[b][:, R:], 0.0)
 
-        groups = [(b, 1) for b in range(BLOCKS)]
+        groups = [(0, EARLY), (EARLY, BLOCKS - EARLY)]
         h_raw = {}
 
-        def load_h(g):
+        def load_h(o, g):
             first, count = groups[g]
-            for o in range(PASSES):
-                raw = keep.tile([P, PACK, count * P], F32, name="h_raw%d%d" % (o, g), tag="h_raw%d%d" % (o, g), align_bytes=64)
-                rows = hT[512 * o : 512 * (o + 1), P * first : P * (first + count)]
-                nc.sync.dma_start(out=raw[:], in_=rows.rearrange("(p j) c -> p j c", j=PACK))
-                h_raw[o, g] = raw
+            raw = keep.tile([P, PACK, count * P], F32, name="h_raw%d%d" % (o, g), tag="h_raw%d%d" % (o, g), align_bytes=64)
+            rows = hT[512 * o : 512 * (o + 1), P * first : P * (first + count)]
+            nc.sync.dma_start(out=raw[:], in_=rows.rearrange("(p j) c -> p j c", j=PACK))
+            h_raw[o, g] = raw
 
-        def load_x(o):
-            nc.sync.dma_start(out=x_tab[o][:], in_=x_words[o].rearrange("p n t -> p (n t)").bitcast(I32))
+        def load_x(o, first, last):
+            words = x_words[o].rearrange("p n t -> p (n t)").bitcast(I32)
+            nc.sync.dma_start(out=x_tab[o][:, first:last], in_=words[:, first:last])
 
         def load_e(o):
             nc.sync.dma_start(out=e_tab[o][:], in_=e_words[o].rearrange("p n t -> p (n t)").bitcast(I32))
 
-        def place_x_scales(first, last):
-            for i in range(first, last):
-                o, q = divmod(i, 4)
-                src = 16 * o + 4 * q
-                dst = 32 * q
-                nc.sync.dma_start(out=xs_mx[o][dst : dst + 4, :].bitcast(I32), in_=xs_got[src : src + 4, :].bitcast(I32))
+        def place_x_scales(o, q, first, last):
+            src = 16 * o + 4 * q
+            dst = 32 * q
+            nc.sync.dma_start(
+                out=xs_mx[o][dst : dst + 4, first:last].bitcast(I32), in_=xs_got[src : src + 4, first:last].bitcast(I32)
+            )
 
         nc.sync.dma_start(offs_t[:], offs)
         nc.sync.dma_start(out=xs_tab[0:32, :].bitcast(I32), in_=x_scales.rearrange("o q c -> (o q) c").bitcast(I32))
-        load_h(0)
-        load_e(0)
+        load_h(0, 0)
+        load_h(1, 0)
+        nc.sync.dma_start(cent_t[:], cent)
         for q in range(4):
             nc.sync.dma_start(out=es_tab[32 * q : 32 * q + 8, :].bitcast(I32), in_=e_scales[:, 4 * q : 4 * q + 4, :].bitcast(I32))
-        nc.sync.dma_start(cent_t[:], cent)
+        load_e(0)
         load_e(1)
-        load_h(1)
         nc.sync.dma_start(cell_t[:], cell)
-        load_h(2)
         nc.vector.tensor_copy(xs_got[:], xs_tab[:].indirect(offs_t[:]))
-        place_x_scales(0, 2)
-        load_x(0)
-        place_x_scales(2, 8)
-        load_x(1)
-        load_h(3)
+        for q in range(2):
+            place_x_scales(0, q, 0, S)
+        load_x(0, 0, T)
+        place_x_scales(0, 2, 0, S)
+        place_x_scales(0, 3, 0, HALF)
+        for q in range(4):
+            place_x_scales(1, q, 0, S if q < 2 else HALF)
+        load_x(1, 0, X_SPLIT)
+        place_x_scales(0, 3, HALF, S)
+        load_x(1, X_SPLIT, T)
+        load_h(0, 1)
+        load_h(1, 1)
+        for q in range(2, 4):
+            place_x_scales(1, q, HALF, S)
 
         es_got = keep.tile([P, R], U8, name="es_got", align_bytes=64)
         e_got = [keep.tile([P, R], U32, name="e_got%d" % o, align_bytes=64) for o in range(PASSES)]
@@ -105,20 +116,18 @@ def tile_picked_yivf_sum_p_kernel(
             nc.vector.tensor_copy(got[:], x_tab[o][:].bitcast(U32).indirect(half_list(offs_t, s)))
             x_got[o, s] = got
 
-        def quantise_h(g, tag):
+        def quantise_h(o, g):
             first, count = groups[g]
-            both = keep.tile([P, PASSES * count * P * PACK], BF16, name="grouped%d" % g, tag=tag, align_bytes=64)
-            for o in range(PASSES):
-                grouped = both[:, o * count * P * PACK : (o + 1) * count * P * PACK]
-                nc.scalar.copy(
-                    grouped.rearrange("p (c i j) -> p c j i", i=4, j=PACK),
-                    h_raw[o, g][:].rearrange("p j (c i) -> p c j i", i=4),
-                )
-                codes = keep.tile([P, count * P], U32, name="h_codes%d%d" % (o, g), align_bytes=64)
-                scales = keep.tile([P, count * P], U8, name="h_scales%d%d" % (o, g), align_bytes=64)
-                nc.vector.quantize_mx(codes[:].bitcast(FP8X4), scales[:], grouped)
-                for i in range(count):
-                    h_mx[o, first + i] = (codes[:, i * P : (i + 1) * P], scales[:, i * P : (i + 1) * P])
+            grouped = keep.tile([P, count * P * PACK], BF16, name="grouped%d%d" % (o, g), align_bytes=64)
+            nc.scalar.copy(
+                grouped[:].rearrange("p (c i j) -> p c j i", i=4, j=PACK),
+                h_raw[o, g][:].rearrange("p j (c i) -> p c j i", i=4),
+            )
+            codes = keep.tile([P, count * P], U32, name="h_codes%d%d" % (o, g), align_bytes=64)
+            scales = keep.tile([P, count * P], U8, name="h_scales%d%d" % (o, g), align_bytes=64)
+            nc.vector.quantize_mx(codes[:].bitcast(FP8X4), scales[:], grouped[:])
+            for i in range(count):
+                h_mx[o, first + i] = (codes[:, i * P : (i + 1) * P], scales[:, i * P : (i + 1) * P])
 
         def one_pass(acc, b, o, codes, scales):
             nc.tensor.matmul_mx(
@@ -131,85 +140,77 @@ def tile_picked_yivf_sum_p_kernel(
                 stop=(o == PASSES - 1),
             )
 
-        def cell_scores(b):
-            acc = psum.tile([P, R], F32, name="z%d" % b, tag="bank%d" % (7 if b == 1 else 6))
+        def cell_scores(b, bank):
+            acc = psum.tile([P, R], F32, name="z%d" % b, tag="bank%d" % bank)
             for o in range(PASSES):
                 one_pass(acc[:], b, o, e_got[o][:], es_got[4 * o : P, :])
             nc.scalar.copy(z_win[b][:, :R], acc[:])
 
-        def store(b, first, res):
-            nc.sync.dma_start(out=out[b * P : (b + 1) * P, first : first + res.shape[1]], in_=res[:])
-
         z_got = {}
 
-        def gather_z(b, s, dst):
-            nc.vector.tensor_copy(dst, z_win[b][:].indirect(half_list(cell_t, s)))
-            z_got[b, s] = dst
+        def gather_z(b, s, on_scalar):
+            got = keep.tile([P, HALF], F32, name="z_got%d%d" % (b, s), align_bytes=64)
+            picked = z_win[b][:].indirect(half_list(cell_t, s))
+            if on_scalar:
+                nc.scalar.activation(got[:], picked, COPY)
+            else:
+                nc.vector.tensor_copy(got[:], picked)
+            z_got[b, s] = got
 
         y_acc = {}
 
-        def scan_pass(o):
+        def y_pass(b, s, o, bank):
+            if o == 0:
+                y_acc[b, s] = psum.tile([P, HALF], F32, name="y%d%d" % (b, s), tag="bank%d" % bank)
+            one_pass(y_acc[b, s][:], b, o, x_got[o, s][:], xs_mx[o][:, s * HALF : (s + 1) * HALF])
+
+        def store(b, s, res):
+            nc.sync.dma_start(out=out[b * P : (b + 1) * P, s * HALF : (s + 1) * HALF], in_=res)
+
+        def sum_on_vector(b, s, res):
+            nc.vector.tensor_tensor(res, y_acc[b, s][:], z_got[b, s][:], ADD)
+            store(b, s, res)
+
+        def sum_on_gpsimd(b, s, y_sb):
+            nc.scalar.copy(y_sb, y_acc[b, s][:])
+            res = keep.tile([P, HALF], F32, name="res%d%d" % (b, s), align_bytes=64)
+            nc.gpsimd.tensor_tensor(res[:], y_sb, z_got[b, s][:], ADD)
+            store(b, s, res[:])
+
+        for o in range(PASSES):
+            quantise_h(o, 0)
+        nc.vector.tensor_copy(es_got[:], es_tab[:].indirect(cent_t[:]))
+        for o in range(PASSES):
+            nc.vector.tensor_copy(e_got[o][:], e_tab[o][:].bitcast(U32).indirect(cent_t[:]))
+        for b in (2, 0, 1):
+            cell_scores(b, 6 + b % 2)
+            for s in range(HALVES):
+                gather_z(b, s, b != 2)
+        for o in range(PASSES):
             for s in range(HALVES):
                 gather_x(o, s)
-                for b in range(3):
-                    if o == 0:
-                        y_acc[b, s] = psum.tile([P, HALF], F32, name="y%d%d" % (b, s), tag="bank%d" % (3 * s + b))
-                    one_pass(y_acc[b, s][:], b, o, x_got[o, s][:], xs_mx[o][:, s * HALF : (s + 1) * HALF])
-
-        quantise_h(0, "grouped0")
-        nc.vector.tensor_copy(e_got[0][:], e_tab[0][:].bitcast(U32).indirect(cent_t[:]))
-        nc.vector.tensor_copy(es_got[:], es_tab[:].indirect(cent_t[:]))
-        nc.vector.tensor_copy(e_got[1][:], e_tab[1][:].bitcast(U32).indirect(cent_t[:]))
-        quantise_h(1, "grouped1")
-        for b in range(2):
-            cell_scores(b)
+        late = BLOCKS - 1
+        for o in range(PASSES):
+            quantise_h(o, 1)
+        cell_scores(late, 6)
+        for o in range(PASSES):
             for s in range(HALVES):
-                tag = "h_raw11" if (b, s) == (0, 1) else "z_got%d%d" % (b, s)
-                early = keep.tile([P, HALF], F32, name="z_got%d%d" % (b, s), tag=tag, align_bytes=64)
-                gather_z(b, s, early[:])
-        quantise_h(2, "z_win0")
-        cell_scores(2)
-        scan_pass(0)
-        between = keep.tile([P, HALF], F32, name="between", tag="xs_got", align_bytes=64)
-        gather_z(2, 0, between[:])
-        scan_pass(1)
-        quantise_h(3, "grouped3")
-
-        def copy_out(b, s, c, width):
-            y_sb = keep.tile([P, width], F32, name="y_sb%d%d" % (b, s), align_bytes=64)
-            nc.scalar.copy(y_sb[:], y_acc[b, s][:, c : c + width])
-            return y_sb
-
-        def sum_on_vector(b, s, c, width):
-            res = keep.tile([P, width], F32, name="res%d_%d" % (b, s * HALF + c), align_bytes=64)
-            nc.vector.tensor_tensor(res[:], y_acc[b, s][:, c : c + width], z_got[b, s][:, c : c + width], ADD)
-            store(b, s * HALF + c, res)
-
-        def sum_on_gpsimd(b, s, c, width):
-            y_sb = copy_out(b, s, c, width)
-            res = keep.tile([P, width], F32, name="res%d_%d" % (b, s * HALF + c), align_bytes=64)
-            nc.gpsimd.tensor_tensor(res[:], y_sb[:], z_got[b, s][:, c : c + width], ADD)
-            store(b, s * HALF + c, res)
-
-        def gather_and_sum(b, s, width):
-            y_sb = copy_out(b, s, 0, HALF)
-            for c in range(0, HALF, width):
-                first = s * HALF + c
-                res = keep.tile([P, width], F32, name="res%d_%d" % (b, first), align_bytes=64)
-                cells = cell_t[:, first // 16 : (first + width) // 16]
-                nc.vector.tensor_tensor(res[:], z_win[b][:].indirect(cells), y_sb[:, c : c + width], ADD)
-                store(b, first, res)
-
-        sum_on_gpsimd(0, 0, 0, HALF)
-        sum_on_vector(1, 0, HALF // 2, HALF // 2)
-        sum_on_gpsimd(1, 0, 0, HALF // 2)
-        sum_on_vector(2, 0, 0, HALF)
-        sum_on_vector(0, 1, 0, HALF)
-        sum_on_vector(1, 1, 0, HALF)
-        gather_and_sum(2, 1, HALF)
-        cell_scores(3)
+                for b in range(EARLY):
+                    y_pass(b, s, o, EARLY * s + b)
         for s in range(HALVES):
-            y_acc[3, s] = psum.tile([P, HALF], F32, name="y3%d" % s, tag="bank%d" % (7 if s == 0 else 0))
+            gather_z(late, s, True)
+        sums = keep.tile([P, BLOCKS * S], F32, name="sums", tag="h_raw11", align_bytes=64)
+
+        def slot(b, s):
+            return sums[:, b * S + s * HALF : b * S + (s + 1) * HALF]
+
+        for s in range(HALVES):
+            for b in range(EARLY):
+                if (b, s) == (EARLY - 1, 0):
+                    sum_on_gpsimd(b, s, slot(b, s))
+                else:
+                    sum_on_vector(b, s, slot(b, s))
+        for s in range(HALVES):
             for o in range(PASSES):
-                one_pass(y_acc[3, s][:], 3, o, x_got[o, s][:], xs_mx[o][:, s * HALF : (s + 1) * HALF])
-            gather_and_sum(3, s, HALF if s == 0 else 256)
+                y_pass(late, s, o, 7 - s)
+            sum_on_vector(late, s, slot(late, s))

@@ -22,8 +22,9 @@ BLOCKS = 4
 EARLY = 3
 HALF = 512
 HALVES = 2
+QUARTER = 256
 Z_WINDOW = 544
-X_SPLIT = 3072
+X_SPLIT = 2048
 
 
 def tile_picked_yivf_sum_p_kernel(
@@ -41,7 +42,7 @@ def tile_picked_yivf_sum_p_kernel(
         e_tab = [keep.tile([P, W], I32, name="e_tab%d" % o, align_bytes=64) for o in range(PASSES)]
         xs_tab = keep.tile([P, T], U8, name="xs_tab", align_bytes=64)
         es_tab = keep.tile([P, W], U8, name="es_tab", align_bytes=64)
-        xs_got = keep.tile([P, S], U8, name="xs_got", align_bytes=64)
+        xs_got = keep.tile([P, S], U8, name="xs_got", tag="xs_got", align_bytes=64)
         xs_mx = [keep.tile([P, S], U8, name="xs_mx%d" % o, align_bytes=64) for o in range(PASSES)]
         z_win = [keep.tile([P, Z_WINDOW], F32, name="z_win%d" % b, align_bytes=64) for b in range(BLOCKS)]
 
@@ -92,16 +93,13 @@ def tile_picked_yivf_sum_p_kernel(
             place_x_scales(0, q, 0, S)
         load_x(0, 0, T)
         place_x_scales(0, 2, 0, S)
-        place_x_scales(0, 3, 0, HALF)
-        for q in range(4):
-            place_x_scales(1, q, 0, S if q < 2 else HALF)
         load_x(1, 0, X_SPLIT)
-        place_x_scales(0, 3, HALF, S)
+        place_x_scales(0, 3, 0, S)
         load_x(1, X_SPLIT, T)
+        for q in range(4):
+            place_x_scales(1, q, 0, S)
         load_h(0, 1)
         load_h(1, 1)
-        for q in range(2, 4):
-            place_x_scales(1, q, HALF, S)
 
         es_got = keep.tile([P, R], U8, name="es_got", align_bytes=64)
         e_got = [keep.tile([P, R], U32, name="e_got%d" % o, align_bytes=64) for o in range(PASSES)]
@@ -129,27 +127,27 @@ def tile_picked_yivf_sum_p_kernel(
             for i in range(count):
                 h_mx[o, first + i] = (codes[:, i * P : (i + 1) * P], scales[:, i * P : (i + 1) * P])
 
-        def one_pass(acc, b, o, codes, scales):
+        def one_pass(acc, b, o, codes, scales, first):
             nc.tensor.matmul_mx(
                 acc,
                 lhsT=h_mx[o, b][0].bitcast(FP8X4),
                 lhsT_scale=h_mx[o, b][1],
                 rhs=codes.bitcast(FP8X4),
                 rhs_scale=scales,
-                start=(o == 0),
-                stop=(o == PASSES - 1),
+                start=first,
+                stop=not first,
             )
 
         def cell_scores(b, bank):
             acc = psum.tile([P, R], F32, name="z%d" % b, tag="bank%d" % bank)
             for o in range(PASSES):
-                one_pass(acc[:], b, o, e_got[o][:], es_got[4 * o : P, :])
+                one_pass(acc[:], b, o, e_got[o][:], es_got[4 * o : P, :], o == 0)
             nc.scalar.copy(z_win[b][:, :R], acc[:])
 
         z_got = {}
 
         def gather_z(b, s, on_scalar):
-            got = keep.tile([P, HALF], F32, name="z_got%d%d" % (b, s), align_bytes=64)
+            got = keep.tile([P, HALF], F32, name="z_got%d%d" % (b, s), tag="z_got%d%d" % (b, s), align_bytes=64)
             picked = z_win[b][:].indirect(half_list(cell_t, s))
             if on_scalar:
                 nc.scalar.activation(got[:], picked, COPY)
@@ -160,22 +158,24 @@ def tile_picked_yivf_sum_p_kernel(
         y_acc = {}
 
         def y_pass(b, s, o, bank):
-            if o == 0:
+            first = (b, s) not in y_acc
+            if first:
                 y_acc[b, s] = psum.tile([P, HALF], F32, name="y%d%d" % (b, s), tag="bank%d" % bank)
-            one_pass(y_acc[b, s][:], b, o, x_got[o, s][:], xs_mx[o][:, s * HALF : (s + 1) * HALF])
+            one_pass(y_acc[b, s][:], b, o, x_got[o, s][:], xs_mx[o][:, s * HALF : (s + 1) * HALF], first)
 
-        def store(b, s, res):
-            nc.sync.dma_start(out=out[b * P : (b + 1) * P, s * HALF : (s + 1) * HALF], in_=res)
+        def store(b, first, res):
+            nc.sync.dma_start(out=out[b * P : (b + 1) * P, first : first + res.shape[1]], in_=res)
 
         def sum_on_vector(b, s, res):
             nc.vector.tensor_tensor(res, y_acc[b, s][:], z_got[b, s][:], ADD)
-            store(b, s, res)
+            store(b, s * HALF, res)
 
-        def sum_on_gpsimd(b, s, y_sb):
-            nc.scalar.copy(y_sb, y_acc[b, s][:])
-            res = keep.tile([P, HALF], F32, name="res%d%d" % (b, s), align_bytes=64)
-            nc.gpsimd.tensor_tensor(res[:], y_sb, z_got[b, s][:], ADD)
-            store(b, s, res[:])
+        def sum_on_gpsimd(b, c, y_sb):
+            width = y_sb.shape[1]
+            nc.scalar.copy(y_sb, y_acc[b, 0][:, c : c + width])
+            res = keep.tile([P, width], F32, name="res%d_%d" % (b, c), align_bytes=64)
+            nc.gpsimd.tensor_tensor(res[:], y_sb, z_got[b, 0][:, c : c + width], ADD)
+            return res
 
         for o in range(PASSES):
             quantise_h(o, 0)
@@ -197,20 +197,31 @@ def tile_picked_yivf_sum_p_kernel(
             for s in range(HALVES):
                 for b in range(EARLY):
                     y_pass(b, s, o, EARLY * s + b)
-        for s in range(HALVES):
-            gather_z(late, s, True)
-        sums = keep.tile([P, BLOCKS * S], F32, name="sums", tag="h_raw11", align_bytes=64)
+        gather_z(late, 0, True)
+        z_third = keep.tile([P, QUARTER], F32, name="z_third", align_bytes=64)
+        nc.scalar.activation(z_third[:], z_win[late][:].indirect(cell_t[:, 2 * QUARTER // 16 : 3 * QUARTER // 16]), COPY)
+        first_sum = keep.tile([P, HALF], F32, name="first_sum", align_bytes=64)
+        sum_on_vector(0, 0, first_sum[:])
+        y_first = keep.tile([P, QUARTER], F32, name="y_first", tag="h_raw01", align_bytes=64)
+        y_next = keep.tile([P, QUARTER + HALF], F32, name="y_next", tag="h_raw11", align_bytes=64)
+        store(1, 0, sum_on_gpsimd(1, 0, y_first[:])[:])
+        store(1, QUARTER, sum_on_gpsimd(1, QUARTER, y_next[:, :QUARTER])[:])
+        slow_sum = sum_on_gpsimd(2, 0, y_next[:, QUARTER:])
+        sums = keep.tile([P, BLOCKS * S], F32, name="sums", tag="h_raw01", align_bytes=64)
 
         def slot(b, s):
             return sums[:, b * S + s * HALF : b * S + (s + 1) * HALF]
 
+        for b in range(EARLY):
+            sum_on_vector(b, 1, slot(b, 1))
+        store(2, 0, slow_sum[:])
+        z_fourth = keep.tile([P, QUARTER], F32, name="z_fourth", tag="z_got11", align_bytes=64)
+        nc.vector.tensor_copy(z_fourth[:], z_win[late][:].indirect(cell_t[:, 3 * QUARTER // 16 :]))
         for s in range(HALVES):
-            for b in range(EARLY):
-                if (b, s) == (EARLY - 1, 0):
-                    sum_on_gpsimd(b, s, slot(b, s))
-                else:
-                    sum_on_vector(b, s, slot(b, s))
-        for s in range(HALVES):
-            for o in range(PASSES):
-                y_pass(late, s, o, 7 - s)
-            sum_on_vector(late, s, slot(late, s))
+            for o in reversed(range(PASSES)):
+                y_pass(late, s, o, 7 if s == 0 else 0)
+        sum_on_vector(late, 0, slot(late, 0))
+        res = slot(late, 1)
+        for c, z_part in ((QUARTER, z_fourth), (0, z_third)):
+            nc.vector.tensor_tensor(res[:, c : c + QUARTER], y_acc[late, 1][:, c : c + QUARTER], z_part[:], ADD)
+            store(late, HALF + c, res[:, c : c + QUARTER])

@@ -22,7 +22,6 @@ BLOCKS = 4
 EARLY = 3
 HALF = 512
 HALVES = 2
-QUARTER = 256
 Z_WINDOW = 544
 X_SPLIT = 2048
 
@@ -96,10 +95,12 @@ def tile_picked_yivf_sum_p_kernel(
         load_x(1, 0, X_SPLIT)
         place_x_scales(0, 3, 0, S)
         load_x(1, X_SPLIT, T)
-        for q in range(4):
-            place_x_scales(1, q, 0, S)
         load_h(0, 1)
+        for q in range(4):
+            place_x_scales(1, q, 0, S if q < 2 else HALF)
         load_h(1, 1)
+        for q in range(2, 4):
+            place_x_scales(1, q, HALF, S)
 
         es_got = keep.tile([P, R], U8, name="es_got", align_bytes=64)
         e_got = [keep.tile([P, R], U32, name="e_got%d" % o, align_bytes=64) for o in range(PASSES)]
@@ -138,10 +139,10 @@ def tile_picked_yivf_sum_p_kernel(
                 stop=not first,
             )
 
-        def cell_scores(b, bank):
+        def cell_scores(b, bank, passes):
             acc = psum.tile([P, R], F32, name="z%d" % b, tag="bank%d" % bank)
-            for o in range(PASSES):
-                one_pass(acc[:], b, o, e_got[o][:], es_got[4 * o : P, :], o == 0)
+            for o in passes:
+                one_pass(acc[:], b, o, e_got[o][:], es_got[4 * o : P, :], o == passes[0])
             nc.scalar.copy(z_win[b][:, :R], acc[:])
 
         z_got = {}
@@ -170,20 +171,13 @@ def tile_picked_yivf_sum_p_kernel(
             nc.vector.tensor_tensor(res, y_acc[b, s][:], z_got[b, s][:], ADD)
             store(b, s * HALF, res)
 
-        def sum_on_gpsimd(b, c, y_sb):
-            width = y_sb.shape[1]
-            nc.scalar.copy(y_sb, y_acc[b, 0][:, c : c + width])
-            res = keep.tile([P, width], F32, name="res%d_%d" % (b, c), align_bytes=64)
-            nc.gpsimd.tensor_tensor(res[:], y_sb, z_got[b, 0][:, c : c + width], ADD)
-            return res
-
         for o in range(PASSES):
             quantise_h(o, 0)
         nc.vector.tensor_copy(es_got[:], es_tab[:].indirect(cent_t[:]))
         for o in range(PASSES):
             nc.vector.tensor_copy(e_got[o][:], e_tab[o][:].bitcast(U32).indirect(cent_t[:]))
         for b in (2, 0, 1):
-            cell_scores(b, 6 + b % 2)
+            cell_scores(b, 6 + b % 2, (0, 1))
             for s in range(HALVES):
                 gather_z(b, s, b != 2)
         for o in range(PASSES):
@@ -192,36 +186,22 @@ def tile_picked_yivf_sum_p_kernel(
         late = BLOCKS - 1
         for o in range(PASSES):
             quantise_h(o, 1)
-        cell_scores(late, 6)
+        cell_scores(late, 6, (1, 0))
         for o in range(PASSES):
             for s in range(HALVES):
                 for b in range(EARLY):
                     y_pass(b, s, o, EARLY * s + b)
-        gather_z(late, 0, True)
-        z_third = keep.tile([P, QUARTER], F32, name="z_third", align_bytes=64)
-        nc.scalar.activation(z_third[:], z_win[late][:].indirect(cell_t[:, 2 * QUARTER // 16 : 3 * QUARTER // 16]), COPY)
-        first_sum = keep.tile([P, HALF], F32, name="first_sum", align_bytes=64)
-        sum_on_vector(0, 0, first_sum[:])
-        y_first = keep.tile([P, QUARTER], F32, name="y_first", tag="h_raw01", align_bytes=64)
-        y_next = keep.tile([P, QUARTER + HALF], F32, name="y_next", tag="h_raw11", align_bytes=64)
-        store(1, 0, sum_on_gpsimd(1, 0, y_first[:])[:])
-        store(1, QUARTER, sum_on_gpsimd(1, QUARTER, y_next[:, :QUARTER])[:])
-        slow_sum = sum_on_gpsimd(2, 0, y_next[:, QUARTER:])
-        sums = keep.tile([P, BLOCKS * S], F32, name="sums", tag="h_raw01", align_bytes=64)
+        for s in range(HALVES):
+            gather_z(late, s, True)
+        sums = keep.tile([P, BLOCKS * S], F32, name="sums", tag="xs_got", align_bytes=64)
 
         def slot(b, s):
             return sums[:, b * S + s * HALF : b * S + (s + 1) * HALF]
 
-        for b in range(EARLY):
-            sum_on_vector(b, 1, slot(b, 1))
-        store(2, 0, slow_sum[:])
-        z_fourth = keep.tile([P, QUARTER], F32, name="z_fourth", tag="z_got11", align_bytes=64)
-        nc.vector.tensor_copy(z_fourth[:], z_win[late][:].indirect(cell_t[:, 3 * QUARTER // 16 :]))
+        for s in range(HALVES):
+            for b in range(EARLY):
+                sum_on_vector(b, s, slot(b, s))
         for s in range(HALVES):
             for o in reversed(range(PASSES)):
                 y_pass(late, s, o, 7 if s == 0 else 0)
-        sum_on_vector(late, 0, slot(late, 0))
-        res = slot(late, 1)
-        for c, z_part in ((QUARTER, z_fourth), (0, z_third)):
-            nc.vector.tensor_tensor(res[:, c : c + QUARTER], y_acc[late, 1][:, c : c + QUARTER], z_part[:], ADD)
-            store(late, HALF + c, res[:, c : c + QUARTER])
+            sum_on_vector(late, s, slot(late, s))

@@ -38,7 +38,7 @@ def tile_picked_yivf_sum_p_kernel(
         cent_t = keep.tile([P, R // 16], U16, name="cent_t")
         cell_t = keep.tile([P, S // 16], U16, name="cell_t")
         x_tab = [keep.tile([P, T], I32, name="x_tab%d" % o, align_bytes=64) for o in range(PASSES)]
-        e_tab = [keep.tile([P, W], I32, name="e_tab%d" % o, align_bytes=64) for o in range(PASSES)]
+        e_tab = keep.tile([P, PASSES * W], I32, name="e_tab", align_bytes=64)
         xs_tab = keep.tile([P, T], U8, name="xs_tab", align_bytes=64)
         es_tab = keep.tile([P, W], U8, name="es_tab", align_bytes=64)
         xs_got = keep.tile([P, S], U8, name="xs_got", tag="xs_got", align_bytes=64)
@@ -67,8 +67,11 @@ def tile_picked_yivf_sum_p_kernel(
             words = x_words[o].rearrange("p n t -> p (n t)").bitcast(I32)
             nc.sync.dma_start(out=x_tab[o][:, first:last], in_=words[:, first:last])
 
-        def load_e(o):
-            nc.sync.dma_start(out=e_tab[o][:], in_=e_words[o].rearrange("p n t -> p (n t)").bitcast(I32))
+        def load_e_scales(queue, first, last):
+            for i in range(first, last):
+                o, q = divmod(i, 4)
+                dst = 32 * q + 4 * o
+                queue.dma_start(out=es_tab[dst : dst + 4, :].bitcast(I32), in_=e_scales[o, 4 * q : 4 * q + 4, :].bitcast(I32))
 
         def place_x_scales(o, q, first, last):
             src = 16 * o + 4 * q
@@ -78,20 +81,20 @@ def tile_picked_yivf_sum_p_kernel(
             )
 
         nc.sync.dma_start(offs_t[:], offs)
-        nc.sync.dma_start(out=xs_tab[0:32, :].bitcast(I32), in_=x_scales.rearrange("o q c -> (o q) c").bitcast(I32))
+        nc.scalar.dma_start(out=xs_tab[0:32, :].bitcast(I32), in_=x_scales.rearrange("o q c -> (o q) c").bitcast(I32))
+        load_e_scales(nc.scalar, 0, 3)
         load_h(0, 0)
         load_h(1, 0)
         nc.sync.dma_start(cent_t[:], cent)
-        for q in range(4):
-            nc.sync.dma_start(out=es_tab[32 * q : 32 * q + 8, :].bitcast(I32), in_=e_scales[:, 4 * q : 4 * q + 4, :].bitcast(I32))
-        load_e(0)
-        load_e(1)
+        nc.sync.dma_start(
+            out=e_tab[:].rearrange("p (o n) -> p o n", o=PASSES), in_=e_words.rearrange("o p n t -> p o (n t)").bitcast(I32)
+        )
+        load_e_scales(nc.sync, 3, 8)
         nc.sync.dma_start(cell_t[:], cell)
         nc.vector.tensor_copy(xs_got[:], xs_tab[:].indirect(offs_t[:]))
-        for q in range(2):
-            place_x_scales(0, q, 0, S)
         load_x(0, 0, T)
-        place_x_scales(0, 2, 0, S)
+        for q in range(3):
+            place_x_scales(0, q, 0, S)
         load_x(1, 0, X_SPLIT)
         place_x_scales(0, 3, 0, S)
         load_x(1, X_SPLIT, T)
@@ -173,9 +176,9 @@ def tile_picked_yivf_sum_p_kernel(
 
         for o in range(PASSES):
             quantise_h(o, 0)
-        nc.vector.tensor_copy(es_got[:], es_tab[:].indirect(cent_t[:]))
         for o in range(PASSES):
-            nc.vector.tensor_copy(e_got[o][:], e_tab[o][:].bitcast(U32).indirect(cent_t[:]))
+            nc.vector.tensor_copy(e_got[o][:], e_tab[:, o * W : (o + 1) * W].bitcast(U32).indirect(cent_t[:]))
+        nc.vector.tensor_copy(es_got[:], es_tab[:].indirect(cent_t[:]))
         for b in (2, 0, 1):
             cell_scores(b, 6 + b % 2, (0, 1))
             for s in range(HALVES):

@@ -24,6 +24,8 @@ HALF = 512
 HALVES = 2
 Z_WINDOW = 544
 X_SPLIT = 2048
+QUADRANTS = (0, 2, 1, 3)
+E_ROWS = 80
 
 
 def tile_picked_yivf_sum_p_kernel(
@@ -40,14 +42,18 @@ def tile_picked_yivf_sum_p_kernel(
         x_tab = [keep.tile([P, T], I32, name="x_tab%d" % o, align_bytes=64) for o in range(PASSES)]
         e_tab = keep.tile([P, PASSES * W], I32, name="e_tab", align_bytes=64)
         xs_tab = keep.tile([P, T], U8, name="xs_tab", align_bytes=64)
-        es_tab = keep.tile([P, W], U8, name="es_tab", align_bytes=64)
+        es_tab = keep.tile([P, PASSES * W], U8, name="es_tab", align_bytes=64)
+        es_got = keep.tile([P, PASSES * R], U8, name="es_got", align_bytes=64)
+        es_mx = keep.tile([P, PASSES * R], U8, name="es_mx", align_bytes=64)
         xs_got = keep.tile([P, S], U8, name="xs_got", tag="xs_got", align_bytes=64)
         xs_mx = [keep.tile([P, S], U8, name="xs_mx%d" % o, align_bytes=64) for o in range(PASSES)]
         z_win = [keep.tile([P, Z_WINDOW], F32, name="z_win%d" % b, align_bytes=64) for b in range(BLOCKS)]
 
-        nc.gpsimd.memset(es_tab[:].bitcast(I32), 0)
+        for first, last in ((0, 64), (64, E_ROWS), (E_ROWS + 16, P)):
+            nc.gpsimd.memset(es_tab[first:last, :].bitcast(I32), 0)
         nc.gpsimd.memset(xs_tab[32:64, :].bitcast(I32), 0)
         nc.vector.memset(xs_tab[64:128, :].bitcast(I32), 0)
+        nc.gpsimd.memset(es_mx[:].bitcast(I32), 0)
         for o in range(PASSES):
             nc.gpsimd.memset(xs_mx[o][:].bitcast(I32), 0)
         for b in range(BLOCKS):
@@ -67,12 +73,6 @@ def tile_picked_yivf_sum_p_kernel(
             words = x_words[o].rearrange("p n t -> p (n t)").bitcast(I32)
             nc.sync.dma_start(out=x_tab[o][:, first:last], in_=words[:, first:last])
 
-        def load_e_scales(queue, first, last):
-            for i in range(first, last):
-                o, q = divmod(i, 4)
-                dst = 32 * q + 4 * o
-                queue.dma_start(out=es_tab[dst : dst + 4, :].bitcast(I32), in_=e_scales[o, 4 * q : 4 * q + 4, :].bitcast(I32))
-
         def place_x_scales(o, q, first, last):
             src = 16 * o + 4 * q
             dst = 32 * q
@@ -80,32 +80,38 @@ def tile_picked_yivf_sum_p_kernel(
                 out=xs_mx[o][dst : dst + 4, first:last].bitcast(I32), in_=xs_got[src : src + 4, first:last].bitcast(I32)
             )
 
+        nc.sync.dma_start(cent_t[:], cent)
+        nc.scalar.dma_start(
+            out=es_tab[E_ROWS : E_ROWS + 16, :].bitcast(I32).rearrange("p (o c) -> p o c", o=PASSES),
+            in_=e_scales.rearrange("o q c -> q o c").bitcast(I32),
+        )
         nc.sync.dma_start(offs_t[:], offs)
         nc.scalar.dma_start(out=xs_tab[0:32, :].bitcast(I32), in_=x_scales.rearrange("o q c -> (o q) c").bitcast(I32))
-        load_e_scales(nc.scalar, 0, 3)
         load_h(0, 0)
         load_h(1, 0)
-        nc.sync.dma_start(cent_t[:], cent)
         nc.sync.dma_start(
             out=e_tab[:].rearrange("p (o n) -> p o n", o=PASSES), in_=e_words.rearrange("o p n t -> p o (n t)").bitcast(I32)
         )
-        load_e_scales(nc.sync, 3, 8)
         nc.sync.dma_start(cell_t[:], cell)
+        for o in range(PASSES):
+            nc.vector.tensor_copy(es_got[:, o * R : (o + 1) * R], es_tab[:, o * W : (o + 1) * W].indirect(cent_t[:]))
         nc.vector.tensor_copy(xs_got[:], xs_tab[:].indirect(offs_t[:]))
+        for q in QUADRANTS:
+            src = E_ROWS + 4 * q
+            nc.sync.dma_start(out=es_mx[32 * q : 32 * q + 4, :].bitcast(I32), in_=es_got[src : src + 4, :].bitcast(I32))
         load_x(0, 0, T)
-        for q in range(3):
+        for q in QUADRANTS[:3]:
             place_x_scales(0, q, 0, S)
         load_x(1, 0, X_SPLIT)
         place_x_scales(0, 3, 0, S)
         load_x(1, X_SPLIT, T)
         load_h(0, 1)
-        for q in range(4):
-            place_x_scales(1, q, 0, S if q < 2 else HALF)
+        for q in QUADRANTS:
+            place_x_scales(1, q, 0, HALF if q % 2 else S)
         load_h(1, 1)
-        for q in range(2, 4):
+        for q in QUADRANTS[2:]:
             place_x_scales(1, q, HALF, S)
 
-        es_got = keep.tile([P, R], U8, name="es_got", align_bytes=64)
         e_got = [keep.tile([P, R], U32, name="e_got%d" % o, align_bytes=64) for o in range(PASSES)]
         x_got = {}
         h_mx = {}
@@ -145,7 +151,7 @@ def tile_picked_yivf_sum_p_kernel(
         def cell_scores(b, bank, passes):
             acc = psum.tile([P, R], F32, name="z%d" % b, tag="bank%d" % bank)
             for o in passes:
-                one_pass(acc[:], b, o, e_got[o][:], es_got[4 * o : P, :], o == passes[0])
+                one_pass(acc[:], b, o, e_got[o][:], es_mx[:, o * R : (o + 1) * R], o == passes[0])
             nc.scalar.copy(z_win[b][:, :R], acc[:])
 
         z_got = {}
@@ -178,7 +184,6 @@ def tile_picked_yivf_sum_p_kernel(
             quantise_h(o, 0)
         for o in range(PASSES):
             nc.vector.tensor_copy(e_got[o][:], e_tab[:, o * W : (o + 1) * W].bitcast(U32).indirect(cent_t[:]))
-        nc.vector.tensor_copy(es_got[:], es_tab[:].indirect(cent_t[:]))
         for b in (2, 0, 1):
             cell_scores(b, 6 + b % 2, (0, 1))
             for s in range(HALVES):

@@ -22,6 +22,7 @@ BLOCKS = 4
 EARLY = 3
 HALF = 512
 HALVES = 2
+QUARTER = 256
 Z_WINDOW = 544
 X_SPLIT = 2048
 QUADRANTS = (0, 2, 1, 3)
@@ -124,18 +125,22 @@ def tile_picked_yivf_sum_p_kernel(
             nc.vector.tensor_copy(got[:], x_tab[o][:].bitcast(U32).indirect(half_list(offs_t, s)))
             x_got[o, s] = got
 
-        def quantise_h(o, g):
+        def quantise_h(g, passes):
             first, count = groups[g]
-            grouped = keep.tile([P, count * P * PACK], BF16, name="grouped%d%d" % (o, g), align_bytes=64)
-            nc.scalar.copy(
-                grouped[:].rearrange("p (c i j) -> p c j i", i=4, j=PACK),
-                h_raw[o, g][:].rearrange("p j (c i) -> p c j i", i=4),
-            )
-            codes = keep.tile([P, count * P], U32, name="h_codes%d%d" % (o, g), align_bytes=64)
-            scales = keep.tile([P, count * P], U8, name="h_scales%d%d" % (o, g), align_bytes=64)
+            width = count * P
+            name = "%d%d" % (g, passes[0])
+            grouped = keep.tile([P, len(passes) * width * PACK], BF16, name="grouped" + name, align_bytes=64)
+            codes = keep.tile([P, len(passes) * width], U32, name="h_codes" + name, align_bytes=64)
+            scales = keep.tile([P, len(passes) * width], U8, name="h_scales" + name, align_bytes=64)
+            for n, o in enumerate(passes):
+                nc.scalar.copy(
+                    grouped[:, n * width * PACK : (n + 1) * width * PACK].rearrange("p (c i j) -> p c j i", i=4, j=PACK),
+                    h_raw[o, g][:].rearrange("p j (c i) -> p c j i", i=4),
+                )
+                for i in range(count):
+                    cols = slice(n * width + i * P, n * width + (i + 1) * P)
+                    h_mx[o, first + i] = (codes[:, cols], scales[:, cols])
             nc.vector.quantize_mx(codes[:].bitcast(FP8X4), scales[:], grouped[:])
-            for i in range(count):
-                h_mx[o, first + i] = (codes[:, i * P : (i + 1) * P], scales[:, i * P : (i + 1) * P])
 
         def one_pass(acc, b, o, codes, scales, first):
             nc.tensor.matmul_mx(
@@ -156,13 +161,15 @@ def tile_picked_yivf_sum_p_kernel(
 
         z_got = {}
 
-        def gather_z(b, s, on_scalar):
-            got = keep.tile([P, HALF], F32, name="z_got%d%d" % (b, s), tag="z_got%d%d" % (b, s), align_bytes=64)
-            picked = z_win[b][:].indirect(half_list(cell_t, s))
-            if on_scalar:
-                nc.scalar.activation(got[:], picked, COPY)
-            else:
-                nc.vector.tensor_copy(got[:], picked)
+        def gather_z(b, s, on_scalar, width):
+            got = keep.tile([P, HALF], F32, name="z_got%d%d" % (b, s), align_bytes=64)
+            for c in range(0, HALF, width):
+                first = s * HALF + c
+                picked = z_win[b][:].indirect(cell_t[:, first // 16 : (first + width) // 16])
+                if on_scalar:
+                    nc.scalar.activation(got[:, c : c + width], picked, COPY)
+                else:
+                    nc.vector.tensor_copy(got[:, c : c + width], picked)
             z_got[b, s] = got
 
         y_acc = {}
@@ -176,40 +183,47 @@ def tile_picked_yivf_sum_p_kernel(
         def store(b, first, res):
             nc.sync.dma_start(out=out[b * P : (b + 1) * P, first : first + res.shape[1]], in_=res)
 
-        def sum_on_vector(b, s, res):
-            nc.vector.tensor_tensor(res, y_acc[b, s][:], z_got[b, s][:], ADD)
-            store(b, s * HALF, res)
+        def sum_on_vector(b, s, c, res):
+            cols = slice(c, c + res.shape[1])
+            nc.vector.tensor_tensor(res, y_acc[b, s][:, cols], z_got[b, s][:, cols], ADD)
+            store(b, s * HALF + c, res)
 
         for o in range(PASSES):
-            quantise_h(o, 0)
+            quantise_h(0, (o,))
         for o in range(PASSES):
             nc.vector.tensor_copy(e_got[o][:], e_tab[:, o * W : (o + 1) * W].bitcast(U32).indirect(cent_t[:]))
         for b in (2, 0, 1):
             cell_scores(b, 6 + b % 2, (0, 1))
             for s in range(HALVES):
-                gather_z(b, s, b != 2)
+                gather_z(b, s, b != 2, HALF)
         for o in range(PASSES):
             for s in range(HALVES):
                 gather_x(o, s)
         late = BLOCKS - 1
-        for o in range(PASSES):
-            quantise_h(o, 1)
+        quantise_h(1, (0, 1))
         cell_scores(late, 6, (1, 0))
         for o in range(PASSES):
             for s in range(HALVES):
                 for b in range(EARLY):
                     y_pass(b, s, o, EARLY * s + b)
         for s in range(HALVES):
-            gather_z(late, s, True)
+            gather_z(late, s, True, HALF if s == 0 else QUARTER)
         sums = keep.tile([P, BLOCKS * S], F32, name="sums", tag="xs_got", align_bytes=64)
 
         def slot(b, s):
             return sums[:, b * S + s * HALF : b * S + (s + 1) * HALF]
 
-        for s in range(HALVES):
-            for b in range(EARLY):
-                sum_on_vector(b, s, slot(b, s))
+        first_sum = keep.tile([P, QUARTER], F32, name="first_sum", align_bytes=64)
+        sum_on_vector(0, 0, 0, first_sum[:])
+        sum_on_vector(0, 0, QUARTER, slot(0, 0)[:, QUARTER:])
+        for c in range(0, HALF, QUARTER):
+            sum_on_vector(1, 0, c, slot(1, 0)[:, c : c + QUARTER])
+        sum_on_vector(2, 0, 0, slot(2, 0))
+        for b in range(EARLY):
+            sum_on_vector(b, 1, 0, slot(b, 1))
         for s in range(HALVES):
             for o in reversed(range(PASSES)):
                 y_pass(late, s, o, 7 if s == 0 else 0)
-            sum_on_vector(late, s, slot(late, s))
+        sum_on_vector(late, 0, 0, slot(late, 0))
+        for c in range(0, HALF, QUARTER):
+            sum_on_vector(late, 1, c, slot(late, 1)[:, c : c + QUARTER])

@@ -23,10 +23,10 @@ EARLY = 3
 HALF = 512
 HALVES = 2
 QUARTER = 256
-Z_WINDOW = 544
-X_SPLIT = 2048
+Z_WINDOW = 272
 QUADRANTS = (0, 2, 1, 3)
-E_ROWS = 80
+E_ROWS = 48
+X_ROWS = 96
 
 
 def tile_picked_yivf_sum_p_kernel(
@@ -50,10 +50,9 @@ def tile_picked_yivf_sum_p_kernel(
         xs_mx = [keep.tile([P, S], U8, name="xs_mx%d" % o, align_bytes=64) for o in range(PASSES)]
         z_win = [keep.tile([P, Z_WINDOW], F32, name="z_win%d" % b, align_bytes=64) for b in range(BLOCKS)]
 
-        for first, last in ((0, 64), (64, E_ROWS), (E_ROWS + 16, P)):
+        nc.vector.memset(xs_tab[:X_ROWS, :].bitcast(I32), 0)
+        for first, last in ((0, E_ROWS), (E_ROWS + 16, P)):
             nc.gpsimd.memset(es_tab[first:last, :].bitcast(I32), 0)
-        nc.gpsimd.memset(xs_tab[32:64, :].bitcast(I32), 0)
-        nc.vector.memset(xs_tab[64:128, :].bitcast(I32), 0)
         nc.gpsimd.memset(es_mx[:].bitcast(I32), 0)
         for o in range(PASSES):
             nc.gpsimd.memset(xs_mx[o][:].bitcast(I32), 0)
@@ -70,12 +69,11 @@ def tile_picked_yivf_sum_p_kernel(
             nc.sync.dma_start(out=raw[:], in_=rows.rearrange("(p j) c -> p j c", j=PACK))
             h_raw[o, g] = raw
 
-        def load_x(o, first, last):
-            words = x_words[o].rearrange("p n t -> p (n t)").bitcast(I32)
-            nc.sync.dma_start(out=x_tab[o][:, first:last], in_=words[:, first:last])
+        def load_x(o):
+            nc.sync.dma_start(out=x_tab[o][:], in_=x_words[o].rearrange("p n t -> p (n t)").bitcast(I32))
 
         def place_x_scales(o, q, first, last):
-            src = 16 * o + 4 * q
+            src = X_ROWS + 16 * o + 4 * q
             dst = 32 * q
             nc.sync.dma_start(
                 out=xs_mx[o][dst : dst + 4, first:last].bitcast(I32), in_=xs_got[src : src + 4, first:last].bitcast(I32)
@@ -87,7 +85,7 @@ def tile_picked_yivf_sum_p_kernel(
             in_=e_scales.rearrange("o q c -> q o c").bitcast(I32),
         )
         nc.sync.dma_start(offs_t[:], offs)
-        nc.scalar.dma_start(out=xs_tab[0:32, :].bitcast(I32), in_=x_scales.rearrange("o q c -> (o q) c").bitcast(I32))
+        nc.scalar.dma_start(out=xs_tab[X_ROWS:, :].bitcast(I32), in_=x_scales.rearrange("o q c -> (o q) c").bitcast(I32))
         load_h(0, 0)
         load_h(1, 0)
         nc.sync.dma_start(
@@ -100,12 +98,10 @@ def tile_picked_yivf_sum_p_kernel(
         for q in QUADRANTS:
             src = E_ROWS + 4 * q
             nc.sync.dma_start(out=es_mx[32 * q : 32 * q + 4, :].bitcast(I32), in_=es_got[src : src + 4, :].bitcast(I32))
-        load_x(0, 0, T)
-        for q in QUADRANTS[:3]:
+        load_x(0)
+        for q in QUADRANTS:
             place_x_scales(0, q, 0, S)
-        load_x(1, 0, X_SPLIT)
-        place_x_scales(0, 3, 0, S)
-        load_x(1, X_SPLIT, T)
+        load_x(1)
         load_h(0, 1)
         for q in QUADRANTS:
             place_x_scales(1, q, 0, HALF if q % 2 else S)
@@ -161,15 +157,15 @@ def tile_picked_yivf_sum_p_kernel(
 
         z_got = {}
 
-        def gather_z(b, s, on_scalar, width):
+        def gather_z(b, s, on_vector):
             got = keep.tile([P, HALF], F32, name="z_got%d%d" % (b, s), align_bytes=64)
-            for c in range(0, HALF, width):
+            for c in range(0, HALF, QUARTER):
                 first = s * HALF + c
-                picked = z_win[b][:].indirect(cell_t[:, first // 16 : (first + width) // 16])
-                if on_scalar:
-                    nc.scalar.activation(got[:, c : c + width], picked, COPY)
+                picked = z_win[b][:].indirect(cell_t[:, first // 16 : (first + QUARTER) // 16])
+                if first < on_vector:
+                    nc.vector.tensor_copy(got[:, c : c + QUARTER], picked)
                 else:
-                    nc.vector.tensor_copy(got[:, c : c + width], picked)
+                    nc.scalar.activation(got[:, c : c + QUARTER], picked, COPY)
             z_got[b, s] = got
 
         y_acc = {}
@@ -195,7 +191,7 @@ def tile_picked_yivf_sum_p_kernel(
         for b in (2, 0, 1):
             cell_scores(b, 6 + b % 2, (0, 1))
             for s in range(HALVES):
-                gather_z(b, s, b != 2, HALF)
+                gather_z(b, s, 3 * QUARTER if b == 2 else 0)
         for o in range(PASSES):
             for s in range(HALVES):
                 gather_x(o, s)
@@ -207,7 +203,7 @@ def tile_picked_yivf_sum_p_kernel(
                 for b in range(EARLY):
                     y_pass(b, s, o, EARLY * s + b)
         for s in range(HALVES):
-            gather_z(late, s, True, HALF if s == 0 else QUARTER)
+            gather_z(late, s, 0)
         sums = keep.tile([P, BLOCKS * S], F32, name="sums", tag="xs_got", align_bytes=64)
 
         def slot(b, s):

@@ -40,22 +40,19 @@ def tile_picked_yivf_sum_p_kernel(
         offs_t = keep.tile([P, S // 16], U16, name="offs_t")
         cent_t = keep.tile([P, R // 16], U16, name="cent_t")
         cell_t = keep.tile([P, S // 16], U16, name="cell_t")
-        x_tab = [keep.tile([P, T], I32, name="x_tab%d" % o, align_bytes=64) for o in range(PASSES)]
-        e_tab = keep.tile([P, PASSES * W], I32, name="e_tab", align_bytes=64)
+        x_tab = {}
+        e_tab = keep.tile([P, PASSES * W], I32, name="e_tab", tag="e_tab", align_bytes=64)
         xs_tab = keep.tile([P, T], U8, name="xs_tab", align_bytes=64)
         es_tab = keep.tile([P, PASSES * W], U8, name="es_tab", align_bytes=64)
         es_got = keep.tile([P, PASSES * R], U8, name="es_got", align_bytes=64)
         es_mx = keep.tile([P, PASSES * R], U8, name="es_mx", align_bytes=64)
         xs_got = keep.tile([P, S], U8, name="xs_got", tag="xs_got", align_bytes=64)
-        xs_mx = [keep.tile([P, S], U8, name="xs_mx%d" % o, align_bytes=64) for o in range(PASSES)]
         z_win = [keep.tile([P, Z_WINDOW], F32, name="z_win%d" % b, align_bytes=64) for b in range(BLOCKS)]
 
         nc.vector.memset(xs_tab[:X_ROWS, :].bitcast(I32), 0)
         for first, last in ((0, E_ROWS), (E_ROWS + 16, P)):
             nc.gpsimd.memset(es_tab[first:last, :].bitcast(I32), 0)
         nc.gpsimd.memset(es_mx[:].bitcast(I32), 0)
-        for o in range(PASSES):
-            nc.gpsimd.memset(xs_mx[o][:].bitcast(I32), 0)
         for b in range(BLOCKS):
             nc.gpsimd.memset(z_win[b][:, R:], 0.0)
 
@@ -69,14 +66,16 @@ def tile_picked_yivf_sum_p_kernel(
             nc.sync.dma_start(out=raw[:], in_=rows.rearrange("(p j) c -> p j c", j=PACK))
             h_raw[o, g] = raw
 
-        def load_x(o):
+        def load_x(o, tag):
+            x_tab[o] = keep.tile([P, T], I32, name="x_tab%d" % o, tag=tag, align_bytes=64)
             nc.sync.dma_start(out=x_tab[o][:], in_=x_words[o].rearrange("p n t -> p (n t)").bitcast(I32))
 
-        def place_x_scales(o, q, first, last):
+        def place_x_scales(queue, o, q, first, last):
             src = X_ROWS + 16 * o + 4 * q
             dst = 32 * q
-            nc.sync.dma_start(
-                out=xs_mx[o][dst : dst + 4, first:last].bitcast(I32), in_=xs_got[src : src + 4, first:last].bitcast(I32)
+            queue.dma_start(
+                out=xs_mx[dst : dst + 4, o * S + first : o * S + last].bitcast(I32),
+                in_=xs_got[src : src + 4, first:last].bitcast(I32),
             )
 
         nc.sync.dma_start(cent_t[:], cent)
@@ -98,16 +97,7 @@ def tile_picked_yivf_sum_p_kernel(
         for q in QUADRANTS:
             src = E_ROWS + 4 * q
             nc.sync.dma_start(out=es_mx[32 * q : 32 * q + 4, :].bitcast(I32), in_=es_got[src : src + 4, :].bitcast(I32))
-        load_x(0)
-        for q in QUADRANTS:
-            place_x_scales(0, q, 0, S)
-        load_x(1)
-        load_h(0, 1)
-        for q in QUADRANTS:
-            place_x_scales(1, q, 0, HALF if q % 2 else S)
-        load_h(1, 1)
-        for q in QUADRANTS[2:]:
-            place_x_scales(1, q, HALF, S)
+        load_x(0, "x_tab0")
 
         e_got = [keep.tile([P, R], U32, name="e_got%d" % o, align_bytes=64) for o in range(PASSES)]
         x_got = {}
@@ -174,7 +164,7 @@ def tile_picked_yivf_sum_p_kernel(
             first = (b, s) not in y_acc
             if first:
                 y_acc[b, s] = psum.tile([P, HALF], F32, name="y%d%d" % (b, s), tag="bank%d" % bank)
-            one_pass(y_acc[b, s][:], b, o, x_got[o, s][:], xs_mx[o][:, s * HALF : (s + 1) * HALF], first)
+            one_pass(y_acc[b, s][:], b, o, x_got[o, s][:], xs_mx[:, o * S + s * HALF : o * S + (s + 1) * HALF], first)
 
         def store(b, first, res):
             nc.sync.dma_start(out=out[b * P : (b + 1) * P, first : first + res.shape[1]], in_=res)
@@ -186,8 +176,21 @@ def tile_picked_yivf_sum_p_kernel(
 
         for o in range(PASSES):
             quantise_h(0, (o,))
+        xs_mx = keep.tile([P, PASSES * S], U8, name="xs_mx", tag="h_raw00", align_bytes=64)
+        nc.gpsimd.memset(xs_mx[:].bitcast(I32), 0)
+        for q in QUADRANTS:
+            place_x_scales(nc.scalar, 0, q, 0, S)
+        for q in QUADRANTS[:2]:
+            place_x_scales(nc.scalar, 1, q, 0, S)
         for o in range(PASSES):
             nc.vector.tensor_copy(e_got[o][:], e_tab[:, o * W : (o + 1) * W].bitcast(U32).indirect(cent_t[:]))
+        load_x(1, "e_tab")
+        load_h(0, 1)
+        for q in QUADRANTS[2:]:
+            place_x_scales(nc.sync, 1, q, 0, HALF)
+        load_h(1, 1)
+        for q in QUADRANTS[2:]:
+            place_x_scales(nc.sync, 1, q, HALF, S)
         for b in (2, 0, 1):
             cell_scores(b, 6 + b % 2, (0, 1))
             for s in range(HALVES):

@@ -27,6 +27,7 @@ Z_WINDOW = 272
 QUADRANTS = (0, 2, 1, 3)
 E_ROWS = 48
 X_ROWS = 96
+PLANE_ROW = (12, 0)
 
 
 def tile_picked_yivf_sum_p_kernel(
@@ -72,9 +73,9 @@ def tile_picked_yivf_sum_p_kernel(
 
         def place_x_scales(queue, o, q, first, last):
             src = X_ROWS + 16 * o + 4 * q
-            dst = 32 * q
+            dst = 32 * q + PLANE_ROW[o]
             queue.dma_start(
-                out=xs_mx[dst : dst + 4, o * S + first : o * S + last].bitcast(I32),
+                out=xs_mx[o][dst : dst + 4, first:last].bitcast(I32),
                 in_=xs_got[src : src + 4, first:last].bitcast(I32),
             )
 
@@ -164,7 +165,7 @@ def tile_picked_yivf_sum_p_kernel(
             first = (b, s) not in y_acc
             if first:
                 y_acc[b, s] = psum.tile([P, HALF], F32, name="y%d%d" % (b, s), tag="bank%d" % bank)
-            one_pass(y_acc[b, s][:], b, o, x_got[o, s][:], xs_mx[:, o * S + s * HALF : o * S + (s + 1) * HALF], first)
+            one_pass(y_acc[b, s][:], b, o, x_got[o, s][:], xs_mx[o][PLANE_ROW[o] :, s * HALF : (s + 1) * HALF], first)
 
         def store(b, first, res):
             nc.sync.dma_start(out=out[b * P : (b + 1) * P, first : first + res.shape[1]], in_=res)
@@ -176,15 +177,19 @@ def tile_picked_yivf_sum_p_kernel(
 
         for o in range(PASSES):
             quantise_h(0, (o,))
-        xs_mx = keep.tile([P, PASSES * S], U8, name="xs_mx", tag="h_raw00", align_bytes=64)
-        nc.gpsimd.memset(xs_mx[:].bitcast(I32), 0)
-        for q in QUADRANTS:
+        xs_mx = [
+            keep.tile([P, S], U8, name="xs_mx0", tag="h_raw00", align_bytes=64),
+            keep.tile([P, S], U8, name="xs_mx1", align_bytes=64),
+        ]
+        nc.vector.tensor_copy(xs_mx[0][:].bitcast(I32), xs_got[:].bitcast(I32))
+        nc.gpsimd.memset(xs_mx[1][:].bitcast(I32), 0)
+        for q in QUADRANTS[:3]:
             place_x_scales(nc.scalar, 0, q, 0, S)
-        for q in QUADRANTS[:2]:
-            place_x_scales(nc.scalar, 1, q, 0, S)
         for o in range(PASSES):
             nc.vector.tensor_copy(e_got[o][:], e_tab[:, o * W : (o + 1) * W].bitcast(U32).indirect(cent_t[:]))
         load_x(1, "e_tab")
+        for q in QUADRANTS[:2]:
+            place_x_scales(nc.sync, 1, q, 0, S)
         load_h(0, 1)
         for q in QUADRANTS[2:]:
             place_x_scales(nc.sync, 1, q, 0, HALF)

@@ -86,12 +86,11 @@ def tile_picked_yivf_sum_p_kernel(
         )
         nc.sync.dma_start(offs_t[:], offs)
         nc.scalar.dma_start(out=xs_tab[X_ROWS:, :].bitcast(I32), in_=x_scales.rearrange("o q c -> (o q) c").bitcast(I32))
+        nc.sync.dma_start(cell_t[:], cell)
         load_h(0, 0)
         load_h(1, 0)
-        nc.sync.dma_start(
-            out=e_tab[:].rearrange("p (o n) -> p o n", o=PASSES), in_=e_words.rearrange("o p n t -> p o (n t)").bitcast(I32)
-        )
-        nc.sync.dma_start(cell_t[:], cell)
+        for o in range(PASSES):
+            nc.sync.dma_start(out=e_tab[:, o * W : (o + 1) * W], in_=e_words[o].rearrange("p n t -> p (n t)").bitcast(I32))
         for o in range(PASSES):
             nc.vector.tensor_copy(es_got[:, o * R : (o + 1) * R], es_tab[:, o * W : (o + 1) * W].indirect(cent_t[:]))
         nc.vector.tensor_copy(xs_got[:], xs_tab[:].indirect(offs_t[:]))
@@ -199,7 +198,7 @@ def tile_picked_yivf_sum_p_kernel(
         for b in (2, 0, 1):
             cell_scores(b, 6 + b % 2, (0, 1))
             for s in range(HALVES):
-                gather_z(b, s, 3 * QUARTER if b == 2 else 0)
+                gather_z(b, s, S if b == 2 else 0)
         for o in range(PASSES):
             for s in range(HALVES):
                 gather_x(o, s)

@@ -27,7 +27,7 @@ Z_WINDOW = 272
 QUADRANTS = (0, 2, 1, 3)
 E_ROWS = 48
 X_ROWS = 96
-PLANE_ROW = (12, 0)
+PLANE_ROW = (12, 4)
 
 
 def tile_picked_yivf_sum_p_kernel(
@@ -178,23 +178,21 @@ def tile_picked_yivf_sum_p_kernel(
             quantise_h(0, (o,))
         xs_mx = [
             keep.tile([P, S], U8, name="xs_mx0", tag="h_raw00", align_bytes=64),
-            keep.tile([P, S], U8, name="xs_mx1", align_bytes=64),
+            keep.tile([P, S], U8, name="xs_mx1", tag="h_raw10", align_bytes=64),
         ]
         nc.vector.tensor_copy(xs_mx[0][:].bitcast(I32), xs_got[:].bitcast(I32))
         nc.gpsimd.memset(xs_mx[1][:].bitcast(I32), 0)
         for q in QUADRANTS[:3]:
             place_x_scales(nc.scalar, 0, q, 0, S)
+        for q in (0, 1):
+            place_x_scales(nc.scalar, 1, q, 0, S)
         for o in range(PASSES):
             nc.vector.tensor_copy(e_got[o][:], e_tab[:, o * W : (o + 1) * W].bitcast(U32).indirect(cent_t[:]))
         load_x(1, "e_tab")
-        for q in QUADRANTS[:2]:
-            place_x_scales(nc.sync, 1, q, 0, S)
-        load_h(0, 1)
-        for q in QUADRANTS[2:]:
-            place_x_scales(nc.sync, 1, q, 0, HALF)
-        load_h(1, 1)
-        for q in QUADRANTS[2:]:
-            place_x_scales(nc.sync, 1, q, HALF, S)
+        for o in range(PASSES):
+            load_h(o, 1)
+            for q in (2, 3):
+                place_x_scales(nc.sync, 1, q, o * HALF, (o + 1) * HALF)
         for b in (2, 0, 1):
             cell_scores(b, 6 + b % 2, (0, 1))
             for s in range(HALVES):

from contextlib import ExitStack

import concourse.mybir as mybir

K, T, S, V, R, W = 1024, 4096, 1024, 512, 256, 1024
FLOPS = 2 * K * V * (S + R)

F32 = mybir.dt.float32
BF16 = mybir.dt.bfloat16
I32 = mybir.dt.int32
U32 = mybir.dt.uint32
U16 = mybir.dt.uint16
U8 = mybir.dt.uint8
FP8X4 = mybir.dt.float8_e4m3fn_x4
ADD = mybir.AluOpType.add
COPY = mybir.ActivationFunctionType.Copy

P = 128
PACK = 4
PASSES = 2
BLOCKS = 4
EARLY = 3
HALF = 512
HALVES = 2
QUARTER = 256
Z_WINDOW = 272
QUADRANTS = (0, 2, 1, 3)
E_ROWS = 48
X_ROWS = 96
PLANE_ROW = (12, 4)


def tile_picked_yivf_sum_p_kernel(
    tc, x_words, x_scales, hT, e_words, e_scales, offs, cent, cell, out
):
    nc = tc.nc
    with ExitStack() as ctx:
        keep = ctx.enter_context(tc.tile_pool(name="keep", bufs=1))
        psum = ctx.enter_context(tc.psum_pool(name="psum", bufs=1))

        offs_t = keep.tile([P, S // 16], U16, name="offs_t")
        cent_t = keep.tile([P, R // 16], U16, name="cent_t")
        cell_t = keep.tile([P, S // 16], U16, name="cell_t")
        x_tab = {}
        e_tab = keep.tile([P, PASSES * W], I32, name="e_tab", tag="e_tab", align_bytes=64)
        xs_tab = keep.tile([P, T], U8, name="xs_tab", align_bytes=64)
        es_tab = keep.tile([P, PASSES * W], U8, name="es_tab", align_bytes=64)
        es_got = keep.tile([P, PASSES * R], U8, name="es_got", align_bytes=64)
        es_mx = keep.tile([P, PASSES * R], U8, name="es_mx", align_bytes=64)
        xs_got = keep.tile([P, S], U8, name="xs_got", tag="xs_got", align_bytes=64)
        z_win = [keep.tile([P, Z_WINDOW], F32, name="z_win%d" % b, align_bytes=64) for b in range(BLOCKS)]

        nc.vector.memset(xs_tab[:X_ROWS, :].bitcast(I32), 0)
        for first, last in ((0, E_ROWS), (E_ROWS + 16, P)):
            nc.gpsimd.memset(es_tab[first:last, :].bitcast(I32), 0)
        nc.gpsimd.memset(es_mx[:].bitcast(I32), 0)
        for b in range(BLOCKS):
            nc.gpsimd.memset(z_win[b][:, R:], 0.0)

        groups = [(0, EARLY), (EARLY, BLOCKS - EARLY)]
        h_raw = {}

        def load_h(o, g):
            first, count = groups[g]
            raw = keep.tile([P, PACK, count * P], F32, name="h_raw%d%d" % (o, g), tag="h_raw%d%d" % (o, g), align_bytes=64)
            rows = hT[512 * o : 512 * (o + 1), P * first : P * (first + count)]
            nc.sync.dma_start(out=raw[:], in_=rows.rearrange("(p j) c -> p j c", j=PACK))
            h_raw[o, g] = raw

        def load_x(o, tag):
            x_tab[o] = keep.tile([P, T], I32, name="x_tab%d" % o, tag=tag, align_bytes=64)
            nc.sync.dma_start(out=x_tab[o][:], in_=x_words[o].rearrange("p n t -> p (n t)").bitcast(I32))

        def place_x_scales(queue, o, q, first, last):
            src = X_ROWS + 16 * o + 4 * q
            dst = 32 * q + PLANE_ROW[o]
            queue.dma_start(
                out=xs_mx[o][dst : dst + 4, first:last].bitcast(I32),
                in_=xs_got[src : src + 4, first:last].bitcast(I32),
            )

        nc.sync.dma_start(cent_t[:], cent)
        nc.scalar.dma_start(
            out=es_tab[E_ROWS : E_ROWS + 16, :].bitcast(I32).rearrange("p (o c) -> p o c", o=PASSES),
            in_=e_scales.rearrange("o q c -> q o c").bitcast(I32),
        )
        nc.sync.dma_start(offs_t[:], offs)
        nc.scalar.dma_start(out=xs_tab[X_ROWS:, :].bitcast(I32), in_=x_scales.rearrange("o q c -> (o q) c").bitcast(I32))
        nc.sync.dma_start(cell_t[:], cell)
        load_h(0, 0)
        load_h(1, 0)
        for o in range(PASSES):
            nc.sync.dma_start(out=e_tab[:, o * W : (o + 1) * W], in_=e_words[o].rearrange("p n t -> p (n t)").bitcast(I32))
        for o in range(PASSES):
            nc.vector.tensor_copy(es_got[:, o * R : (o + 1) * R], es_tab[:, o * W : (o + 1) * W].indirect(cent_t[:]))
        nc.vector.tensor_copy(xs_got[:], xs_tab[:].indirect(offs_t[:]))
        for q in QUADRANTS:
            src = E_ROWS + 4 * q
            nc.sync.dma_start(out=es_mx[32 * q : 32 * q + 4, :].bitcast(I32), in_=es_got[src : src + 4, :].bitcast(I32))
        load_x(0, "x_tab0")

        e_got = [keep.tile([P, R], U32, name="e_got%d" % o, align_bytes=64) for o in range(PASSES)]
        x_got = {}
        h_mx = {}

        def half_list(t, s):
            return t[:, s * HALF // 16 : (s + 1) * HALF // 16]

        def gather_x(o, s):
            got = keep.tile([P, HALF], U32, name="x_got%d%d" % (o, s), align_bytes=64)
            nc.vector.tensor_copy(got[:], x_tab[o][:].bitcast(U32).indirect(half_list(offs_t, s)))
            x_got[o, s] = got

        def quantise_h(g, passes):
            first, count = groups[g]
            width = count * P
            name = "%d%d" % (g, passes[0])
            grouped = keep.tile([P, len(passes) * width * PACK], BF16, name="grouped" + name, align_bytes=64)
            codes = keep.tile([P, len(passes) * width], U32, name="h_codes" + name, align_bytes=64)
            scales = keep.tile([P, len(passes) * width], U8, name="h_scales" + name, align_bytes=64)
            for n, o in enumerate(passes):
                nc.scalar.copy(
                    grouped[:, n * width * PACK : (n + 1) * width * PACK].rearrange("p (c i j) -> p c j i", i=4, j=PACK),
                    h_raw[o, g][:].rearrange("p j (c i) -> p c j i", i=4),
                )
                for i in range(count):
                    cols = slice(n * width + i * P, n * width + (i + 1) * P)
                    h_mx[o, first + i] = (codes[:, cols], scales[:, cols])
            nc.vector.quantize_mx(codes[:].bitcast(FP8X4), scales[:], grouped[:])

        def one_pass(acc, b, o, codes, scales, first):
            nc.tensor.matmul_mx(
                acc,
                lhsT=h_mx[o, b][0].bitcast(FP8X4),
                lhsT_scale=h_mx[o, b][1],
                rhs=codes.bitcast(FP8X4),
                rhs_scale=scales,
                start=first,
                stop=not first,
            )

        def cell_scores(b, bank, passes):
            acc = psum.tile([P, R], F32, name="z%d" % b, tag="bank%d" % bank)
            for o in passes:
                one_pass(acc[:], b, o, e_got[o][:], es_mx[:, o * R : (o + 1) * R], o == passes[0])
            nc.scalar.copy(z_win[b][:, :R], acc[:])

        z_got = {}

        def gather_z(b, s, on_vector):
            got = keep.tile([P, HALF], F32, name="z_got%d%d" % (b, s), align_bytes=64)
            for c in range(0, HALF, QUARTER):
                first = s * HALF + c
                picked = z_win[b][:].indirect(cell_t[:, first // 16 : (first + QUARTER) // 16])
                if first < on_vector:
                    nc.vector.tensor_copy(got[:, c : c + QUARTER], picked)
                else:
                    nc.scalar.activation(got[:, c : c + QUARTER], picked, COPY)
            z_got[b, s] = got

        y_acc = {}

        def y_pass(b, s, o, bank):
            first = (b, s) not in y_acc
            if first:
                y_acc[b, s] = psum.tile([P, HALF], F32, name="y%d%d" % (b, s), tag="bank%d" % bank)
            one_pass(y_acc[b, s][:], b, o, x_got[o, s][:], xs_mx[o][PLANE_ROW[o] :, s * HALF : (s + 1) * HALF], first)

        def store(b, first, res):
            nc.sync.dma_start(out=out[b * P : (b + 1) * P, first : first + res.shape[1]], in_=res)

        def sum_on_vector(b, s, c, res):
            cols = slice(c, c + res.shape[1])
            nc.vector.tensor_tensor(res, y_acc[b, s][:, cols], z_got[b, s][:, cols], ADD)
            store(b, s * HALF + c, res)

        for o in range(PASSES):
            quantise_h(0, (o,))
        xs_mx = [
            keep.tile([P, S], U8, name="xs_mx0", tag="h_raw00", align_bytes=64),
            keep.tile([P, S], U8, name="xs_mx1", tag="h_raw10", align_bytes=64),
        ]
        nc.vector.tensor_copy(xs_mx[0][:].bitcast(I32), xs_got[:].bitcast(I32))
        nc.gpsimd.memset(xs_mx[1][:].bitcast(I32), 0)
        for q in QUADRANTS[:3]:
            place_x_scales(nc.scalar, 0, q, 0, S)
        for q in (0, 1):
            place_x_scales(nc.scalar, 1, q, 0, S)
        for o in range(PASSES):
            nc.vector.tensor_copy(e_got[o][:], e_tab[:, o * W : (o + 1) * W].bitcast(U32).indirect(cent_t[:]))
        load_x(1, "e_tab")
        for o in range(PASSES):
            load_h(o, 1)
            for q in (2, 3):
                place_x_scales(nc.sync, 1, q, o * HALF, (o + 1) * HALF)
        for b in (2, 0, 1):
            cell_scores(b, 6 + b % 2, (0, 1))
            for s in range(HALVES):
                gather_z(b, s, S if b == 2 else 0)
        for o in range(PASSES):
            for s in range(HALVES):
                gather_x(o, s)
        late = BLOCKS - 1
        quantise_h(1, (0, 1))
        cell_scores(late, 6, (1, 0))
        for o in range(PASSES):
            for s in range(HALVES):
                for b in range(EARLY):
                    y_pass(b, s, o, EARLY * s + b)
        for s in range(HALVES):
            gather_z(late, s, 0)
        sums = keep.tile([P, BLOCKS * S], F32, name="sums", tag="xs_got", align_bytes=64)

        def slot(b, s):
            return sums[:, b * S + s * HALF : b * S + (s + 1) * HALF]

        first_sum = keep.tile([P, QUARTER], F32, name="first_sum", align_bytes=64)
        sum_on_vector(0, 0, 0, first_sum[:])
        sum_on_vector(0, 0, QUARTER, slot(0, 0)[:, QUARTER:])
        for c in range(0, HALF, QUARTER):
            sum_on_vector(1, 0, c, slot(1, 0)[:, c : c + QUARTER])
        sum_on_vector(2, 0, 0, slot(2, 0))
        for b in range(EARLY):
            sum_on_vector(b, 1, 0, slot(b, 1))
        for s in range(HALVES):
            for o in reversed(range(PASSES)):
                y_pass(late, s, o, 7 if s == 0 else 0)
        sum_on_vector(late, 0, 0, slot(late, 0))
        for c in range(0, HALF, QUARTER):
            sum_on_vector(late, 1, c, slot(late, 1)[:, c : c + QUARTER])
